import numpy as np, ml_dtypes
CORES = [24,25,26,27,28,29,30,31]
N = 8
import mx_ref
BF = ml_dtypes.bfloat16
def gentries(a):
    return np.ascontiguousarray(a.reshape(8, 16, -1).transpose(0, 2, 1)).reshape(8, -1)
def gtable(e):
    e = np.asarray(e); return np.ascontiguousarray(e.reshape(8, -1, 16).transpose(0, 2, 1)).reshape(128, -1).astype(np.int32)
def gcols(t, e):
    v = np.concatenate([t.reshape(8, 16, -1, 4), np.zeros((8, 16, 1, 4), BF)], axis=2)
    return np.ascontiguousarray(np.stack([v[g][:, e[g]] for g in range(8)])).reshape(128, -1)
def tile(rs):
    return np.stack(rs, axis=2).reshape(128, -1).astype(BF)
def pick(q, e):
    c = np.concatenate([q[0].reshape(128, -1, 4), np.zeros((128, 1, 4), np.uint8)], axis=1); s = np.concatenate([q[1], np.ones((16, 1), np.uint8)], axis=1)
    return (np.ascontiguousarray(c[:, e].reshape(128, -1)), np.ascontiguousarray(s[:, e]))
def join(*qs):
    return (np.concatenate([q[0] for q in qs], axis=1), np.concatenate([q[1] for q in qs], axis=1))
def put(q, e, v):
    c, s = q[0].reshape(128, -1, 4).copy(), q[1].copy(); c[:, e] = v[0].reshape(128, -1, 4); s[:, e] = v[1]
    return (c.reshape(128, -1), s)
def pk(c, s):
    return (np.ascontiguousarray(c), mx_ref.live(s))
def emit(q):
    return q[0], q[1]
def packed(v, rng):
    q = [mx_ref.quantize(np.ascontiguousarray(v[r])) for r in range(N)]
    return np.stack([a for a, b in q]), np.stack([mx_ref.plane(b, rng) for a, b in q])
def values_of_codes():
    e, c = np.zeros((128, 128, 4), np.float32), np.zeros((128, 2, 4), np.uint8)
    e[np.arange(128), np.arange(128), 0] = 1
    c[:127, :, 0] = np.arange(256).reshape(2, 128).T[:127]
    return mx_ref.matmul(mx_ref.quantize(e.reshape(128, 512).astype(BF)), (c.reshape(128, 8), np.full((16, 2), 127, np.uint8))).T.reshape(-1).astype(np.float64)
CODE_VALUE, SCALE_VALUE = values_of_codes(), 2.0 ** (np.arange(256) - 127.0)
def decode(q):
    return (CODE_VALUE[q[0]].reshape(16, 8, -1, 4) * SCALE_VALUE[q[1]][:, None, :, None] + 0.0).reshape(128, -1).astype(np.float32)
def f(rng, *shape):
    return mx_ref.flush((rng.standard_normal(shape, dtype=np.float32) * np.exp2(rng.integers(-2, 3, shape[:-1] + (1,)))).astype(BF))
def wide(rng, *shape, cols=0):
    v = rng.standard_normal(shape, dtype=np.float32) * np.exp2(rng.integers(-12, 13, shape)).astype(np.float32)
    if cols: v *= np.repeat(np.exp2(rng.integers(-cols, cols + 1, shape[:-2] + (1, shape[-1] // 4))) * (rng.random(shape[:-2] + (1, shape[-1] // 4)) > 0.0625), 4, axis=-1).astype(np.float32)
    return mx_ref.flush(v.astype(BF))
C, H = 320, 160
MASK = [1, 2, 4]
def numbers_of(rng):
    return {"x": np.array(f(rng, N, 128, 4 * C)), "u": np.array(f(rng, N, 128, 512)), "v": np.array(f(rng, N, 128, 512))}
def stored(l, k):
    return {"gl": np.stack([gtable(l[r]) for r in range(N)]), "gk": np.stack([gtable(k[r]) for r in range(N)])}
def lists(rng):
    e = np.tile(np.arange(C), (N, 8, 1))
    return stored(rng.permuted(e, axis=2), rng.permuted(e, axis=2))
def layers(rng, still=[]):
    w = np.array(f(rng, N, 128, 2048)).reshape(N, 8, 16, 4, 8, 16, 4)
    for i in still:
        w[:, :, i] = 0
        w[:, :, :, :, :, i] = 0
    return w
def weights(rng, w):
    c, p = packed(np.ascontiguousarray(w).reshape(N, 128, 2048), rng)
    return {"wc": c, "ws": p}
def setup_inputs(rng):
    return {**numbers_of(rng), **lists(rng), **weights(rng, layers(rng))}
def setup_inputs_ties(rng):
    d = numbers_of(rng)
    o = rng.permutation(N)
    k = rng.integers(-1, 2, (N, 8, C, 2)).astype(np.float32)
    k[o[1]] = 1
    k[o[2]] = -1
    x = d["x"].reshape(N, 8, 16, C, 4)
    x[:, :, 0] = 0
    x[:, :, 0, :, :2] = k.astype(BF)
    a = np.exp2(rng.integers(-3, 4, 8).astype(np.float32))[None, :, None]
    x[:, :, 8:] = 0
    x[:, :, 8, :, 0] = (-1.125 * a).astype(BF)
    x[:, :, 10, :, 0] = (-0.0703125 * a).astype(BF)
    c = np.ones(N, np.float32)
    c[o[0]] = 0
    u = d["u"].reshape(N, 128, 128, 4)
    for t in range(2):
        u[:, :, t::16] = 0
        for h in range(0, 128, 16): u[:, h, h + t, t] = c.astype(BF)
    w = layers(rng, [0])
    w[:, :, :, :, :, 8:] = 0
    for g in range(8):
        w[:, g, 8, 0, g, 8, 0] = -28.0
        for b in range(4): w[:, g, 10, b, g, 9, 0] = -2.0 ** (b - 5)
    return {"x": x.reshape(N, 128, 4 * C), "u": u.reshape(N, 128, 512), "v": d["v"], **stored(rng.integers(0, C, (N, 8, C)), rng.integers(0, C, (N, 8, C))), **weights(rng, w)}
def setup_inputs_near(rng):
    d = numbers_of(rng)
    o = rng.permutation(N) % 2
    k = np.where(o == 0, 2.0 ** -30, 1.0).astype(np.float32)
    x = d["x"].astype(np.float32).reshape(N, 8, 16, C, 4)
    x[:, :, :8] = 0
    s = rng.integers(-1, 2, (N, 8, C, 2)) * k[:, None, None, None]
    x[:, :, 0, :, :2] = 1.125 * s
    x[:, :, 1, :, :2] = -1.25 * s
    x[:, :, 3, :, :2] = rng.choice([-1.0, 1.0], (N, 8, C, 2)) * 2.0 ** -30
    x[:, :, 5] = 2.0 ** -30
    for r in range(N):
        for g in rng.permutation(8)[:4]: x[r, g, 0, rng.integers(C), 0] = 2.0 ** 30 * rng.choice([-1.0, 1.0])
    u = d["u"].reshape(N, 128, 128, 4)
    w = layers(rng, range(8))
    for t in range(2):
        u[:, :, t::16] = 0
        for h in range(0, 128, 16):
            u[:, h, h + t, t] = (1.125 * k).astype(BF)
            u[:, h + 1, h + t, t] = k.astype(BF)
            u[:, h + 2, h + t, t] = k.astype(BF)
        for g in range(8):
            w[:, g, 3, t, g, 2, t] = 2.0 ** -8
            w[:, g, 3, t, g, 4, t] = 32.0
    return {"x": x.reshape(N, 128, 4 * C).astype(BF), "u": u.reshape(N, 128, 512), "v": d["v"], **lists(rng), **weights(rng, w)}
def setup_inputs_odd(rng):
    d = numbers_of(rng)
    x = (1.0 + (2 * rng.integers(0, 64, (N, 16, 8, C, 4)) + 1) * 2.0 ** -7) * np.exp2(-rng.integers(0, 7, (N, 16, 8, C, 4)).astype(np.float64)) * rng.choice([-1.0, 1.0], (N, 16, 8, C, 4))
    x[:, :, 0, :, 0] = 1.96875 * 2.0 ** 8 * rng.choice([-1.0, 1.0], (N, 16, C))
    x[:, ::2, 1, :, :2] = rng.integers(7, 10, (N, 8, C, 2)) * 2.0 ** -8
    x[:, ::2, 2, :, :2] = 2.0 ** -5
    u = d["u"].reshape(N, 16, 8, 128, 4)
    for t in range(2):
        u[:, :, :, t::16] = 0
        for g in range(8):
            u[:, 2 * g, 1, 16 * g + t, t] = 1.0
            u[:, 2 * g, 2, 16 * g + t, t] = -1.0
    return {"x": x.astype(np.float32).reshape(N, 128, 4 * C).astype(BF), "u": u.reshape(N, 128, 512), "v": d["v"], **lists(rng), **weights(rng, layers(rng, [0, 1, 2, 8]))}
def setup_inputs_ends(rng):
    d = numbers_of(rng)
    x = np.zeros((N, 128, C, 4))
    u = d["u"].astype(np.float32).reshape(N, 128, 128, 4)
    v = d["v"].astype(np.float32)
    w = np.zeros((N, 128, 4, 128, 4), np.float32)
    o, e = rng.permutation(N) % 4, rng.permutation(N) % 4
    i = np.arange(128)
    def amount(large, *n):
        return (0.9 + 0.1 * rng.random(n)) * 2.0 ** 30 if large else (1.0 + 0.125 * rng.integers(0, 8, n)) * 2.0 ** -30
    for r in range(N):
        large = o[r] < 2
        if o[r] == 3: x[r] = d["x"][r].astype(np.float32).reshape(128, C, 4)[:, :1]
        else: x[r] = -amount(large, 128, C, 4) * (0.5 if large else 1.0)
        if o[r] == 1: x[r] *= rng.choice([-1.0, 1.0], (1, C, 1))
        x[r, 7::8] = 2.0 ** -30
        for t in range(2):
            h = rng.permutation(8)
            c = np.where(h < 2, 0.0, h % 2 * 2.0 - 1.0)[None, :, None]
            if o[r] == 3: u[r, :, t::16] *= np.abs(c).astype(np.float32)
            else: u[r, :, t::16] = c * amount(large, 128, 8, 4)
        v[r] = rng.choice([-1.0, 1.0], (128, 512)) * amount(large, 128, 512)
        k = np.array([1.0, 2.0, 4.0])[rng.permutation(8) % 3][i // 16]
        k[7::8] = 0
        if o[r] == 2: k = np.where(i % 8 == 7, 2.0 ** 8, 2.0 ** -8)
        for b in range(4): w[r, i, b, i, b] = k
    both = []
    for z in (e, (e + rng.integers(1, 4)) % 4):
        a = rng.integers(0, C, (N, 8, C))
        a[z == 0] = C - 1
        a[z == 1] = 0
        a[z == 2] = rng.integers(0, 2, a[z == 2].shape) * (C - 1)
        both.append(a)
    return {"x": x.astype(np.float32).reshape(N, 128, 4 * C).astype(BF), "u": u.reshape(N, 128, 512).astype(BF), "v": v.astype(BF), **stored(*both), **weights(rng, w.astype(BF))}
def setup_inputs_spread(rng):
    d = setup_inputs(rng)
    d["x"] = wide(rng, N, 128, 4 * C, cols=6)
    return d
def check_inputs(d):
    b = []
    for k in ("x", "u", "v"):
        a = np.abs(d[k].astype(np.float32))
        if not (np.isfinite(a).all() and ((a == 0) | (a >= 2.0 ** -30) & (a <= 2.0 ** 30)).all()): b.append("a value of " + k)
    for k in ("gl", "gk"):
        if not ((d[k] >= 0) & (d[k] < C)).all(): b.append("an entry of " + k)
    none, least, most = [emit(mx_ref.quantize(np.full((128, 16), k, np.float32).astype(BF)))[1][0, 0] for k in (0.0, 2.0 ** -8, 2.0 ** 8)]
    for r in range(N):
        if ((d["wc"][r] == 0x7F) | (d["wc"][r] == 0xFF)).any(): b.append("wc: a code that is no number")
        s = mx_ref.live(d["ws"][r])
        if ((s != none) & ((s < least) | (s > most))).any(): b.append("ws: a scale out of range")
        if (((d["wc"][r].reshape(16, 8, 512, 4) & 0x7F) != 0) & (s == none)[:, None, :, None]).any(): b.append("wc: a code other than zero under the scale of zeros")
    return b
def at(t, e):
    return np.take_along_axis(t, e, axis=1)
def reference(x, u, v, gl, gk, wc, ws):
    qu = [mx_ref.quantize(u[r]) for r in range(N)]
    lay = [pk(wc[r], ws[r]) for r in range(N)]
    left, right = [gentries(gl[r]) for r in range(N)], [gentries(gk[r]) for r in range(N)]
    now = [x[r] for r in range(N)]
    for mask in MASK:
        point, made, sent, turn = [], [], [], []
        for r in range(N):
            l, k = left[r], right[r]
            s = mx_ref.matmul(qu[r], mx_ref.quantize(now[r]))
            b = s[::16] > 0
            turn.append(s[1::16][:, :H] < 0)
            state, down = b, []
            for t in range(3):
                a, c = at(state, l), at(state, k)
                down.append(np.where(a, l, np.where(c, k, np.arange(C))))
                state = b ^ (a & ~c)
            o = at(down[0], at(down[1], down[2]))
            z = (gcols(now[r], o).astype(np.float32) + gcols(now[r], at(l, o)).astype(np.float32)) * np.float32(0.5)
            q = mx_ref.quantize(z.astype(BF))
            h = tile([mx_ref.matmul(pick(lay[r], np.arange(128 * b, 128 * b + 128)), q) * np.float32(0.03125) for b in range(4)])
            point.append(o)
            made.append(h)
            sent.append(decode(mx_ref.quantize(h)).astype(BF))
        for r in range(N):
            p = r ^ mask
            l, k = left[r], right[r]
            m = at(point[p], k)
            add = np.concatenate([gcols(sent[p], m[:, :H]), gcols(made[r], m[:, H:])], axis=1)
            now[r] = (now[r].astype(np.float32) + add.astype(np.float32)).astype(BF)
            t = np.concatenate([turn[r], turn[r]], axis=1)
            left[r] = np.where(t, np.roll(k, H, axis=1), l)
            right[r] = np.where(t, np.roll(l, H, axis=1), k)
    y, lr = np.zeros((N, 128, C), np.float32), np.zeros((N, 8, 2 * C), np.float32)
    oc, osc = np.zeros((N, 128, 4 * C), np.uint8), np.zeros((N, 16, C), np.uint8)
    for r in range(N):
        q = mx_ref.quantize(now[r])
        y[r] = mx_ref.matmul(mx_ref.quantize(v[r]), q)
        lr[r] = np.concatenate([left[r], right[r]], axis=1)
        oc[r], osc[r] = emit(q)
    return {"y": y, "lr": lr, "oc": oc, "osc": osc}

@@ -1,0 +1,401 @@
+from concourse.bass import DstId, RemoteDMATransfer
+from concourse.mybir import dt, AluOpType, ActivationFunctionType
+
+MASKS = [1, 2, 4]
+C, HALF = 320, 160
+CODES, U8, BF, F32, I32, U16 = "float8_e4m3fn_x4", "uint8", "bfloat16", "float32", "int32", "uint16"
+SCRATCH = {}
+for _n, _w, _d in [
+    ("X", 1280, BF), ("X2", 1280, BF), ("Y", 1280, BF), ("Z", 1280, BF), ("H", 1280, BF), ("HP", 640, BF),
+    ("xq", 320, CODES), ("xs", 320, U8), ("zq", 320, CODES), ("zs", 320, U8),
+    ("ut", 512, BF), ("uq", 128, CODES), ("us", 128, U8), ("up", 256, CODES), ("upl", 256, U8), ("uo", 16, U16), ("ui", 16, I32),
+    ("vt", 512, BF), ("vq", 128, CODES), ("vs", 128, U8), ("wq", 512, CODES), ("wsb", 512, U8),
+    ("et", 2048, BF), ("eq", 512, CODES), ("es", 512, U8), ("one", 512, BF),
+    ("it", 320, F32), ("kd", 320, I32), ("ke", 320, I32), ("km", 320, BF), ("k16", 320, F32), ("k4", 320, F32),
+    ("pi", 8, I32), ("pc", 8, F32), ("ci", 20, I32), ("cc", 40, I32),
+    ("lk", 40, I32), ("lx", 40, I32), ("l4", 80, U16), ("dkl", 80, I32),
+    ("bb", 320, BF), ("tk", 320, BF), ("tk1", 320, BF), ("tk2", 320, BF), ("M", 320, BF), ("G1", 320, BF), ("G2", 320, F32),
+    ("sm", 320, BF), ("s1", 320, F32), ("s2", 320, F32), ("so", 320, F32), ("sx", 320, F32), ("sl", 320, F32),
+    ("mi", 20, I32), ("m7", 20, I32), ("gi", 20, I32), ("g2", 20, I32), ("m2", 40, I32), ("by", 80, I32), ("qq", 40, I32), ("qy", 80, I32), ("sy", 80, I32),
+    ("q1", 40, I32), ("sb", 120, I32), ("sb2", 60, I32), ("pr", 80, I32), ("ps", 40, I32), ("pd", 40, I32), ("d01", 40, U16),
+    ("pr2", 40, I32), ("ps2", 20, I32), ("pd2", 20, I32), ("d2", 20, U16),
+    ("R1", 320, F32), ("R2", 320, F32), ("O", 320, F32), ("o4", 80, U16), ("MR", 320, F32), ("lrep", 640, F32),
+    ("tu", 160, BF), ("st", 160, BF), ("tt", 20, I32), ("xd", 20, I32), ("xt", 20, I32), ("ysb", 320, F32),
+]:
+    SCRATCH[_n] = ("sbuf", [128, _w], _d)
+for _r in range(3):
+    SCRATCH["hq%d" % _r] = ("sbuf", [128, HALF], CODES)
+    SCRATCH["hs%d" % _r] = ("sbuf", [128, HALF], U8)
+    SCRATCH["lc%d" % _r] = ("sbuf", [128, HALF], CODES)
+    SCRATCH["ls%d" % _r] = ("sbuf", [128, HALF], U8)
+    SCRATCH["kp%d" % _r] = ("sbuf", [128, 20], U16)
+    SCRATCH["mq%d" % _r] = ("sbuf", [128, 40], U16)
+    SCRATCH["m4%d" % _r] = ("sbuf", [128, 80], U16)
+for _r in range(4):
+    SCRATCH["lko%d" % _r] = ("sbuf", [128, 40], U16)
+PSUM = ["PA", "PB", "PT", "PY", "P0", "P1", "P2", "P3"]
+for _n in PSUM:
+    SCRATCH[_n] = ("psum", [128, 512], F32)
+DMASEMS = ["dm%d" % i for i in range(40)]
+SEMAPHORES = ["qv", "qs", "qt", "qg", "rl"] + ["ak%d" % r for r in range(3)] + ["am%d" % r for r in range(3)] + ["ah%d" % r for r in range(3)] + DMASEMS
+
+
+def rank_program(g, core, T, topo):
+    rank = T.rank_of(core)
+    if rank is None:
+        return
+    A, F = AluOpType, ActivationFunctionType
+    Q = {"v": g.vector, "s": g.scalar, "t": g.tensor, "g": g, "y": g.sync}
+    SEM = {"v": "qv", "s": "qs", "t": "qt", "g": "qg"}
+    count, known, clock, hist, total = {}, {q: {} for q in Q}, {}, {}, {}
+
+    def region(v):
+        if v[0] == "ind":
+            raise ValueError("indirect")
+        if len(v) == 4:
+            return v[0], v[1], v[2], (v[3], v[1] % v[3])
+        return v[0], v[1], v[2], None
+
+    def meets(p, q):
+        if p[1] >= q[2] or q[1] >= p[2]:
+            return False
+        return not (p[3] and q[3] and p[3][0] == q[3][0] and p[3][1] != q[3][1])
+
+    def regions(views):
+        out = []
+        for v in views:
+            if v is None:
+                continue
+            if v[0] == "ind":
+                out += [region(v[1]), region(v[2])]
+            else:
+                out.append(region(v))
+        return out
+
+    def prepare(q, reads, writes):
+        toks = {}
+        for rs, iswrite in ((regions(reads), False), (regions(writes), True)):
+            for p in rs:
+                for (h, w, tok) in hist.get(p[0], []):
+                    if (iswrite or w or p[0] in PSUM) and meets(p, h):
+                        toks[tok[0]] = max(toks.get(tok[0], 0), tok[1])
+        todo = [(s, n) for s, n in toks.items() if known[q].get(s, 0) < n]
+        keep = [t for t in todo if not any(o != t and clock[o].get(t[0], 0) >= t[1] for o in todo)]
+        for s, n in keep:
+            Q[q].wait_ge(T.sem[s], n)
+            for a, b in clock[(s, n)].items():
+                known[q][a] = max(known[q].get(a, 0), b)
+
+    def record(tok, q, reads, writes):
+        ck = dict(known[q]) if q else {}
+        ck[tok[0]] = tok[1]
+        clock[tok] = ck
+        total[tok[0]] = max(total.get(tok[0], 0), tok[1])
+        for p in regions(writes):
+            hist[p[0]] = [h for h in hist.get(p[0], []) if not (p[3] is None and p[1] <= h[0][1] and h[0][2] <= p[2])]
+            hist[p[0]].append((p, True, tok))
+        for p in regions(reads):
+            hist.setdefault(p[0], []).append((p, False, tok))
+
+    def op(q, fn, reads, writes):
+        prepare(q, reads, writes)
+        s = SEM[q]
+        count[s] = count.get(s, 0) + 1
+        fn().then_inc(T.sem[s], 1)
+        record((s, count[s]), q, reads, writes)
+
+    ndma = [0]
+
+    def dma(q, out, in_, reads, writes):
+        prepare(q, reads, writes)
+        s = DMASEMS[ndma[0]]
+        ndma[0] += 1
+        Q[q].dma_start(out, in_).then_inc(T.sem[s], 16)
+        record((s, 16), q, reads, writes)
+
+    def ap(v):
+        if v[0] == "ind":
+            return ap(v[1]).indirect(ap(v[2]))
+        return T[v[0]][:, v[1]:v[2]] if len(v) == 3 else T[v[0]][:, v[1]:v[2]:v[3]]
+
+    def byt(v):
+        return ap(v).bitcast(dt.uint8)
+
+    def copy(out, in_):
+        op("v", lambda: g.vector.tensor_copy(ap(out), ap(in_)), [in_], [out])
+
+    def tt(out, a, b, o):
+        op("v", lambda: g.vector.tensor_tensor(ap(out), ap(a), ap(b), o), [a, b], [out])
+
+    def ts(out, a, s1, o1, s2=None, o2=None):
+        rd = [a] + [s for s in (s1, s2) if isinstance(s, tuple)]
+        p1, p2 = [ap(s) if isinstance(s, tuple) else s for s in (s1, s2)]
+        if o2 is None:
+            op("v", lambda: g.vector.tensor_scalar(ap(out), ap(a), p1, None, o1), rd, [out])
+        else:
+            op("v", lambda: g.vector.tensor_scalar(ap(out), ap(a), p1, p2, o1, o2), rd, [out])
+
+    def scan(out, k, v):
+        op("v", lambda: g.vector.tensor_tensor_scan(ap(out), ap(k), ap(v), 0.0, A.add, A.max), [k, v], [out])
+
+    def act(out, in_, scale=None, bias=None):
+        if scale is None:
+            fn = lambda: g.scalar.activation(ap(out), ap(in_), F.Copy)
+        elif bias is None:
+            fn = lambda: g.scalar.activation(ap(out), ap(in_), F.Identity, scale=scale)
+        else:
+            fn = lambda: g.scalar.activation(ap(out), ap(in_), F.Identity, bias=bias, scale=scale)
+        op("s", fn, [in_], [out])
+
+    def quant(q, s, v):
+        op("v", lambda: g.vector.quantize_mx(ap(q), ap(s), ap(v)), [v], [q, s])
+
+    def mx(out, wq, ws, xq, xs):
+        op("t", lambda: g.tensor.matmul_mx(ap(out), ap(wq), ap(ws), ap(xq), ap(xs), True, True), [wq, ws, xq, xs], [out])
+
+    def iota(out, pattern, base, cm, small=False):
+        if small:
+            fn = lambda: g.iota(ap(out), pattern, base, cm, allow_small_or_imprecise_dtypes=True)
+        else:
+            fn = lambda: g.iota(ap(out), pattern, base, cm)
+        op("g", fn, [], [out])
+
+    def fill(out, c):
+        op("v", lambda: g.vector.memset(ap(out), c), [], [out])
+
+    def off4(out, s, v):
+        scan(s, ("k4", 0, C), v)
+        ts(out, (s[0], 3, C, 4), 4.0, A.mult, ("pc", 0, 1), A.add)
+
+    def land(buf, width, sem, n):
+        record((sem, n), None, [], [(b, 0, width) for b in buf])
+
+    def send(dst, sem, out, in_, reads):
+        prepare("g", reads, [])
+        rid, pid, _ = topo.addr(dst)
+        m = topo.mask(core, dst)
+        g.remote_dma(out, in_, T.sem[sem], T.sem.rl, pid=pid, routing_id=rid, dma_engine_mask=m)
+        total["rl"] = total.get("rl", 0) + len(topo.engines(core, dst))
+
+    partner = [T.cores[rank ^ m] for m in MASKS]
+    for r in range(3):
+        e = len(topo.engines(partner[r], core))
+        land(["kp%d" % r], 20, "ak%d" % r, e)
+        land(["mq%d" % r], 40, "am%d" % r, e)
+        land(["lc%d" % r, "ls%d" % r], HALF, "ah%d" % r, 2 * e)
+
+    dma("y", ap(("lk", 0, 20)), T.gl[:, :], [], [("lk", 0, 20)])
+    dma("s", ap(("lk", 20, 30)), T.gk[:, 10:20], [], [("lk", 20, 30)])
+    dma("s", ap(("lk", 30, 40)), T.gk[:, 0:10], [], [("lk", 30, 40)])
+    dma("y", ap(("ut", 0, 512)), T.u[:, :], [], [("ut", 0, 512)])
+    dma("s", ap(("X", 640, 1280)), T.x[:, 640:1280], [], [("X", 640, 1280)])
+    dma("y", ap(("X", 0, 640)), T.x[:, 0:640], [], [("X", 0, 640)])
+    dma("s", ap(("X2", 640, 1280)), T.x[:, 640:1280], [], [("X2", 640, 1280)])
+    dma("y", byt(("wq", 0, 512)), T.wc[:, :], [], [("wq", 0, 512)])
+    dma("y", ap(("wsb", 0, 512)), T.ws[:, :], [], [("wsb", 0, 512)])
+    dma("y", ap(("vt", 0, 512)), T.v[:, :], [], [("vt", 0, 512)])
+
+    iota(("pi", 0, 1), [[0, 1]], 0, 1)
+    iota(("ui", 0, 16), [[1, 2], [16, 8]], 0, 0)
+    iota(("ci", 0, 20), [[16, 20]], 0, 0)
+    iota(("it", 0, C), [[1, C]], 0, 0, True)
+    iota(("ke", 0, C), [[4, C]], 131, -1)
+    iota(("kd", 0, C), [[1, C]], 128, -1)
+    ts(("pi", 1, 2), ("pi", 0, 1), 3, A.bitwise_and)
+    ts(("pi", 2, 3), ("pi", 0, 1), 12, A.bitwise_and)
+    ts(("pi", 3, 4), ("pi", 0, 1), 15, A.bitwise_and)
+    ts(("pc", 2, 3), ("pi", 2, 3), 1024.0, A.mult, -12288.0, A.add)
+    copy(("pc", 1, 2), ("pi", 1, 2))
+    copy(("pc", 3, 4), ("pi", 3, 4))
+    tt(("pc", 0, 1), ("pc", 1, 2), ("pc", 2, 3), A.add)
+    copy(("uo", 0, 16), ("ui", 0, 16))
+    ts(("cc", 0, 20), ("ci", 0, 20), ("pc", 3, 4), A.add)
+    ts(("cc", 20, 40), ("ci", 0, 20), ("pc", 3, 4), A.add)
+    fill(("one", 0, 512), 1.0)
+
+    def lists(r):
+        n = "lko%d" % r
+        copy((n, 20, 30), ("lk", 30, 40))
+        copy((n, 30, 40), ("lk", 20, 30))
+        copy((n, 0, 20), ("lk", 0, 20))
+
+    def differences():
+        tt(("dkl", 40, 60), ("lk", 0, 20), ("cc", 0, 20), A.subtract)
+        tt(("dkl", 60, 80), ("lk", 0, 20), ("cc", 0, 20), A.subtract)
+        for a in (0, 20):
+            tt(("dkl", a, a + 10), ("lk", 30, 40), ("cc", 0, 10), A.subtract)
+            tt(("dkl", a + 10, a + 20), ("lk", 20, 30), ("cc", 10, 20), A.subtract)
+
+    def send_k(r):
+        n = "lko%d" % r
+        send(partner[r], "ak%d" % r, T["kp%d" % r][:, :], ap((n, 20, 40)), [(n, 20, 40)])
+
+    lists(0)
+    send_k(0)
+    for b in range(4):
+        op("g", lambda: g.affine_select(ap(("et", 512 * b, 512 * b + 512)), ap(("one", 0, 512)), [[-1, 512]], A.is_equal, 0.0, b, 4),
+           [("one", 0, 512)], [("et", 512 * b, 512 * b + 512)])
+    act(("lrep", 0, C), ("ind", ("it", 0, C), ("lko0", 0, 20)))
+    ts(("ke", 0, C), ("ke", 0, C), 12, A.bitwise_and)
+    ts(("k4", 0, C), ("ke", 0, C), 0.0, A.is_equal, -9216.0, A.mult)
+    ts(("k4", 0, C), ("k4", 0, C), 1024.0, A.add)
+    off4(("l4", 0, 80), ("sl", 0, C), ("lrep", 0, C))
+    quant(("uq", 0, 128), ("us", 0, 128), ("ut", 0, 512))
+    op("v", lambda: g.vector.tensor_copy(T.up[:, 0:256].bitcast(dt.uint32), T.uq[:, 0:128].bitcast(dt.uint32).indirect(T.uo[:, 0:16])),
+       [("uq", 0, 128), ("uo", 0, 16)], [("up", 0, 256)])
+    op("s", lambda: g.scalar.activation(T.upl[:, 0:256], T.us[:, 0:128].indirect(T.uo[:, 0:16]), F.Copy),
+       [("us", 0, 128), ("uo", 0, 16)], [("upl", 0, 256)])
+
+    UP, UT, US, VT = ("up", 0, 128), ("upl", 0, 128), ("up", 128, 256), ("upl", 128, 256)
+
+    def upper_signs():
+        mx(("PB", 0, HALF), UP, UT, ("xq", HALF, C), ("xs", HALF, C))
+
+    def upper_b():
+        ts(("bb", HALF, C), ("PB", 0, HALF), 0.0, A.is_gt, 2.0, A.mult)
+
+    quant(("xq", HALF, C), ("xs", HALF, C), ("X", 640, 1280))
+    upper_signs()
+
+    def y_piece(i):
+        a = 320 * i
+        tt(("Y", a, a + 320), ("ind", ("X", 0, 1280), ("l4", 20 * i, 20 * i + 20)), ("X2", a, a + 320), A.add)
+
+    for r in range(3):
+        lko, m4, dst = "lko%d" % r, "m4%d" % r, partner[r]
+        L, K = (lko, 0, 20), (lko, 20, 40)
+        quant(("xq", 0, HALF), ("xs", 0, HALF), ("X", 0, 640))
+        mx(("PA", 0, HALF), UP, UT, ("xq", 0, HALF), ("xs", 0, HALF))
+        mx(("PT", 0, HALF), US, VT, ("xq", 0, HALF), ("xs", 0, HALF))
+        act(("X2", 0, 640), ("X", 0, 640))
+        if r == 0:
+            upper_b()
+        y_piece(2)
+        ts(("bb", 0, HALF), ("PA", 0, HALF), 0.0, A.is_gt, 2.0, A.mult)
+        act(("tk", 0, C), ("ind", ("bb", 0, C), K), -0.5, 2.0)
+        if r == 0:
+            ts(("kd", 0, C), ("kd", 0, C), 15, A.bitwise_and)
+            ts(("k16", 0, C), ("kd", 0, C), 0.0, A.is_equal, -135168.0, A.mult)
+            ts(("km", 0, C), ("kd", 0, C), 0.0, A.is_equal, -264.0, A.mult)
+            ts(("k16", 0, C), ("k16", 0, C), 4096.0, A.add)
+            ts(("km", 0, C), ("km", 0, C), 8.0, A.add)
+            differences()
+        else:
+            y_piece(3)
+        tt(("M", 0, C), ("ind", ("bb", 0, C), L), ("tk", 0, C), A.add)
+        act(("tk1", 0, C), ("ind", ("M", 0, C), K), 8.0)
+        y_piece(0)
+        tt(("G1", 0, C), ("ind", ("M", 0, C), L), ("tk1", 0, C), A.add)
+        act(("tk2", 0, C), ("ind", ("G1", 0, C), K), 64.0)
+        scan(("s1", 0, C), ("k16", 0, C), ("G1", 0, C))
+        scan(("sm", 0, C), ("km", 0, C), ("M", 0, C))
+        copy(("gi", 0, 20), ("s1", 15, C, 16))
+        copy(("mi", 0, 20), ("sm", 15, C, 16))
+        tt(("G2", 0, C), ("ind", ("G1", 0, C), L), ("tk2", 0, C), A.add)
+        A0, A1, B0, B1 = [("sb", a, a + 20) for a in (40, 60, 80, 100)]
+        ts(("m7", 0, 20), ("mi", 0, 20), 7, A.bitwise_and)
+        ts(B0, ("mi", 0, 20), 1, A.bitwise_and)
+        ts(("qq", 0, 20), ("gi", 0, 20), 2, A.logical_shift_right, 1, A.bitwise_and)
+        ts(("qq", 20, 40), ("gi", 0, 20), 5, A.logical_shift_right, 1, A.bitwise_and)
+        ts(A0, ("m7", 0, 20), 3.0, A.is_ge)
+        tt(B1, ("qq", 20, 40), B0, A.not_equal)
+        tt(A1, ("qq", 0, 20), A0, A.not_equal)
+        scan(("s2", 0, C), ("k16", 0, C), ("G2", 0, C))
+        tt(("sb", 0, 40), ("sb", 80, 120), ("sb", 40, 80), A.is_gt)
+        copy(("g2", 0, 20), ("s2", 15, C, 16))
+        tt(("pr", 0, 80), ("sb", 0, 80), ("dkl", 0, 80), A.mult)
+        ts(("m2", 0, 20), ("gi", 0, 20), 7, A.bitwise_and)
+        ts(("m2", 20, 40), ("gi", 0, 20), 3, A.logical_shift_right, 7, A.bitwise_and)
+        tt(("ps", 0, 40), ("pr", 0, 40), ("pr", 40, 80), A.add)
+        ts(("by", 40, 60), ("gi", 0, 20), 1, A.bitwise_and)
+        ts(("by", 60, 80), ("gi", 0, 20), 3, A.logical_shift_right, 1, A.bitwise_and)
+        tt(("pd", 0, 40), ("ps", 0, 40), ("cc", 0, 40), A.add)
+        ts(("by", 0, 40), ("m2", 0, 40), 3.0, A.is_ge)
+        for i, s in enumerate((2, 8, 5, 11)):
+            ts(("qy", 20 * i, 20 * i + 20), ("g2", 0, 20), s, A.logical_shift_right, 1, A.bitwise_and)
+        copy(("d01", 0, 40), ("pd", 0, 40))
+        act(("R1", 0, C), ("ind", ("it", 0, C), ("d01", 0, 20)))
+        act(("R2", 0, C), ("ind", ("R1", 0, C), ("d01", 20, 40)))
+        tt(("sy", 0, 80), ("qy", 0, 80), ("by", 0, 80), A.not_equal)
+        tt(("q1", 0, 40), ("sy", 0, 40), ("sy", 40, 80), A.is_gt)
+        tt(("sb2", 20, 40), ("q1", 0, 20), A0, A.not_equal)
+        tt(("sb2", 40, 60), ("q1", 20, 40), B0, A.not_equal)
+        tt(("sb2", 0, 20), ("sb2", 40, 60), ("sb2", 20, 40), A.is_gt)
+        tt(("pr2", 0, 40), ("sb2", 0, 40), ("dkl", 20, 60), A.mult)
+        tt(("ps2", 0, 20), ("pr2", 0, 20), ("pr2", 20, 40), A.add)
+        tt(("pd2", 0, 20), ("ps2", 0, 20), ("cc", 0, 20), A.add)
+        copy(("d2", 0, 20), ("pd2", 0, 20))
+        if r == 0:
+            y_piece(3)
+        y_piece(1)
+        act(("O", HALF, C), ("ind", ("R2", 0, C), ("d2", 10, 20)))
+        copy(("O", 0, HALF), ("ind", ("R2", 0, C), ("d2", 0, 10)))
+        off4(("o4", 0, 80), ("so", 0, C), ("O", 0, C))
+        act(("MR", 0, C), ("ind", ("O", 0, C), ("kp%d" % r, 0, 20)))
+        act(("Z", 640, 1280), ("ind", ("Y", 0, 1280), ("o4", 40, 80)), 0.5)
+        ts(("Z", 0, 640), ("ind", ("Y", 0, 1280), ("o4", 0, 40)), 0.5, A.mult)
+        quant(("zq", 0, C), ("zs", 0, C), ("Z", 0, 1280))
+        off4((m4, 0, 80), ("sx", 0, C), ("MR", 0, C))
+        send(dst, "am%d" % r, T["mq%d" % r][:, :], ap((m4, 40, 80)), [(m4, 40, 80)])
+        for b in range(4):
+            mx(("P%d" % b, 0, C), ("wq", 128 * b, 128 * b + 128), ("wsb", 128 * b, 128 * b + 128), ("zq", 0, C), ("zs", 0, C))
+        ts(("H", 0, 1280, 4), ("P0", 0, C), 0.03125, A.mult)
+        act(("H", 1, 1280, 4), ("P1", 0, C), 0.03125)
+        ts(("H", 2, 1280, 4), ("P2", 0, C), 0.03125, A.mult)
+        act(("H", 3, 1280, 4), ("P3", 0, C), 0.03125)
+        act(("HP", 320, 640), ("ind", ("H", 0, 1280), (m4, 20, 40)))
+        copy(("HP", 0, 320), ("ind", ("H", 0, 1280), (m4, 0, 20)))
+        hq, hs = ("hq%d" % r, 0, HALF), ("hs%d" % r, 0, HALF)
+        quant(hq, hs, ("HP", 0, 640))
+        send(dst, "ah%d" % r, T["lc%d" % r][:, 0:HALF].bitcast(dt.uint8), byt(hq), [hq])
+        send(dst, "ah%d" % r, T["ls%d" % r][:, 0:HALF], ap(hs), [hs])
+        tt(("X", 640, 1280), ("ind", ("H", 0, 1280), ("mq%d" % r, 0, 40)), ("X", 640, 1280), A.add)
+        quant(("xq", HALF, C), ("xs", HALF, C), ("X", 640, 1280))
+        if r < 2:
+            act(("X2", 640, 1280), ("X", 640, 1280))
+        ts(("tu", 0, HALF), ("PT", 0, HALF), 0.0, A.is_lt)
+        if r < 2:
+            upper_signs()
+        else:
+            quant(("vq", 0, 128), ("vs", 0, 128), ("vt", 0, 512))
+            mx(("PY", 0, HALF), ("vq", 0, 128), ("vs", 0, 128), ("xq", HALF, C), ("xs", HALF, C))
+        tt(("xd", 0, 20), ("lk", 20, 40), ("lk", 0, 20), A.subtract)
+        scan(("st", 0, HALF), ("km", 0, HALF), ("tu", 0, HALF))
+        if r < 2:
+            upper_b()
+        copy(("tt", 0, 10), ("st", 15, HALF, 16))
+        copy(("tt", 10, 20), ("st", 15, HALF, 16))
+        ts(("tt", 0, 20), ("tt", 0, 20), 1, A.bitwise_and)
+        tt(("xt", 0, 20), ("tt", 0, 20), ("xd", 0, 20), A.mult)
+        tt(("lk", 0, 20), ("lk", 0, 20), ("xt", 0, 20), A.add)
+        tt(("lk", 20, 40), ("lk", 20, 40), ("xt", 0, 20), A.subtract)
+        lists(r + 1)
+        n = "lko%d" % (r + 1)
+        act(("lrep", 0, C), ("ind", ("it", 0, C), (n, 0, 20)))
+        if r < 2:
+            send_k(r + 1)
+            differences()
+            off4(("l4", 0, 80), ("sl", 0, C), ("lrep", 0, C))
+        else:
+            act(("lrep", C, 2 * C), ("ind", ("it", 0, C), (n, 20, 40)))
+            act(("ysb", HALF, C), ("PY", 0, HALF))
+            dma("y", T.y[:, HALF:C], ap(("ysb", HALF, C)), [("ysb", HALF, C)], [])
+            dma("y", T.oc[:, 4 * HALF:4 * C], byt(("xq", HALF, C)), [("xq", HALF, C)], [])
+            for k in range(4):
+                dma("y", T.osc[4 * k:4 * k + 4, HALF:C], T.xs[32 * k:32 * k + 4, HALF:C], [("xs", HALF, C)], [])
+            dma("y", T.lr[:, :], T.lrep[::16, :], [("lrep", 0, 2 * C)], [])
+        if r == 0:
+            quant(("eq", 0, 512), ("es", 0, 512), ("et", 0, 2048))
+        for b in range(4):
+            mx(("P%d" % b, 0, HALF), ("eq", 128 * b, 128 * b + 128), ("es", 128 * b, 128 * b + 128), ("lc%d" % r, 0, HALF), ("ls%d" % r, 0, HALF))
+        for b in range(4):
+            tt(("X", b, 640, 4), ("P%d" % b, 0, HALF), ("X", b, 640, 4), A.add)
+    quant(("xq", 0, HALF), ("xs", 0, HALF), ("X", 0, 640))
+    mx(("PA", 0, HALF), ("vq", 0, 128), ("vs", 0, 128), ("xq", 0, HALF), ("xs", 0, HALF))
+    dma("y", T.oc[:, 0:4 * HALF], byt(("xq", 0, HALF)), [("xq", 0, HALF)], [])
+    for k in range(4):
+        dma("y" if k % 2 else "s", T.osc[4 * k:4 * k + 4, 0:HALF], T.xs[32 * k:32 * k + 4, 0:HALF], [("xs", 0, HALF)], [])
+    copy(("ysb", 0, HALF), ("PA", 0, HALF))
+    dma("y", T.y[:, 0:HALF], ap(("ysb", 0, HALF)), [("ysb", 0, HALF)], [])
+    for s in sorted(total):
+        g.wait_ge(T.sem[s], total[s])

@@ -1,8 +1,8 @@
-from concourse.bass import DstId, RemoteDMATransfer
 from concourse.mybir import dt, AluOpType, ActivationFunctionType
 
 MASKS = [1, 2, 4]
 C, HALF = 320, 160
+YV = 0
 CODES, U8, BF, F32, I32, U16 = "float8_e4m3fn_x4", "uint8", "bfloat16", "float32", "int32", "uint16"
 SCRATCH = {}
 for _n, _w, _d in [
@@ -11,16 +11,16 @@ for _n, _w, _d in [
     ("ut", 512, BF), ("uq", 128, CODES), ("us", 128, U8), ("up", 256, CODES), ("upl", 256, U8), ("uo", 16, U16), ("ui", 16, I32),
     ("vt", 512, BF), ("vq", 128, CODES), ("vs", 128, U8), ("wq", 512, CODES), ("wsb", 512, U8),
     ("et", 2048, BF), ("eq", 512, CODES), ("es", 512, U8), ("one", 512, BF),
-    ("it", 320, F32), ("kd", 320, I32), ("ke", 320, I32), ("km", 320, BF), ("k16", 320, F32), ("k4", 320, F32),
-    ("pi", 8, I32), ("pc", 8, F32), ("ci", 20, I32), ("cc", 40, I32),
-    ("lk", 40, I32), ("lx", 40, I32), ("l4", 80, U16), ("dkl", 80, I32),
-    ("bb", 320, BF), ("tk", 320, BF), ("tk1", 320, BF), ("tk2", 320, BF), ("M", 320, BF), ("G1", 320, BF), ("G2", 320, F32),
+    ("it", 320, F32), ("it3", 1536, F32), ("kd", 320, I32), ("ke", 320, I32), ("km", 320, BF), ("k16", 320, F32), ("k4", 320, F32),
+    ("pi", 8, I32), ("pc", 8, F32), ("ci", 20, I32), ("base", 40, I32), ("q0", 40, I32), ("pst", 40, I32),
+    ("l4", 80, U16), ("bbK", 320, BF), ("bbL", 320, BF), ("own", 320, BF), ("tk", 320, BF), ("M", 320, BF),
+    ("tk1", 320, F32), ("G1", 320, F32), ("tk2", 320, F32), ("G2", 320, F32),
     ("sm", 320, BF), ("s1", 320, F32), ("s2", 320, F32), ("so", 320, F32), ("sx", 320, F32), ("sl", 320, F32),
-    ("mi", 20, I32), ("m7", 20, I32), ("gi", 20, I32), ("g2", 20, I32), ("m2", 40, I32), ("by", 80, I32), ("qq", 40, I32), ("qy", 80, I32), ("sy", 80, I32),
-    ("q1", 40, I32), ("sb", 120, I32), ("sb2", 60, I32), ("pr", 80, I32), ("ps", 40, I32), ("pd", 40, I32), ("d01", 40, U16),
-    ("pr2", 40, I32), ("ps2", 20, I32), ("pd2", 20, I32), ("d2", 20, U16),
-    ("R1", 320, F32), ("R2", 320, F32), ("O", 320, F32), ("o4", 80, U16), ("MR", 320, F32), ("lrep", 640, F32),
-    ("tu", 160, BF), ("st", 160, BF), ("tt", 20, I32), ("xd", 20, I32), ("xt", 20, I32), ("ysb", 320, F32),
+    ("mi", 20, I32), ("gi", 20, I32), ("g2", 20, I32), ("qy", 80, I32), ("q1", 40, I32), ("ab0", 40, I32), ("ab1", 40, I32),
+    ("u0", 40, I32), ("cs", 40, I32), ("sn", 40, I32), ("ev", 40, I32), ("pr1", 40, I32), ("cs1", 40, I32), ("pr2", 40, I32), ("cs2", 40, I32),
+    ("dm0", 20, I32), ("dm1", 20, I32), ("da1", 20, I32), ("dm2", 20, I32), ("da2", 20, I32), ("d0", 20, U16), ("d1", 20, U16), ("d2", 20, U16),
+    ("sg", 160, BF), ("sgt", 160, BF), ("R1", 320, F32), ("R2", 320, F32), ("O", 320, F32), ("o4", 80, U16), ("MR", 320, F32),
+    ("lrep", 640, F32), ("tu", 160, BF), ("st", 160, BF), ("tt", 20, F32), ("xd", 20, I32), ("xt", 20, I32), ("ysb", 320, F32),
 ]:
     SCRATCH[_n] = ("sbuf", [128, _w], _d)
 for _r in range(3):
@@ -28,16 +28,16 @@ for _r in range(3):
     SCRATCH["hs%d" % _r] = ("sbuf", [128, HALF], U8)
     SCRATCH["lc%d" % _r] = ("sbuf", [128, HALF], CODES)
     SCRATCH["ls%d" % _r] = ("sbuf", [128, HALF], U8)
-    SCRATCH["kp%d" % _r] = ("sbuf", [128, 20], U16)
-    SCRATCH["mq%d" % _r] = ("sbuf", [128, 40], U16)
+    SCRATCH["ar%d" % _r] = ("sbuf", [128, 64], U16)
     SCRATCH["m4%d" % _r] = ("sbuf", [128, 80], U16)
 for _r in range(4):
     SCRATCH["lko%d" % _r] = ("sbuf", [128, 40], U16)
+    SCRATCH["lk%d" % _r] = ("sbuf", [128, 40], I32)
 PSUM = ["PA", "PB", "PT", "PY", "P0", "P1", "P2", "P3"]
 for _n in PSUM:
     SCRATCH[_n] = ("psum", [128, 512], F32)
 DMASEMS = ["dm%d" % i for i in range(40)]
-SEMAPHORES = ["qv", "qs", "qt", "qg", "rl"] + ["ak%d" % r for r in range(3)] + ["am%d" % r for r in range(3)] + ["ah%d" % r for r in range(3)] + DMASEMS
+SEMAPHORES = ["qv", "qs", "qt", "qg", "rl"] + [a + str(r) for a in ("ak", "am", "ah") for r in range(3)] + DMASEMS
 
 
 def rank_program(g, core, T, topo):
@@ -47,14 +47,11 @@ def rank_program(g, core, T, topo):
     A, F = AluOpType, ActivationFunctionType
     Q = {"v": g.vector, "s": g.scalar, "t": g.tensor, "g": g, "y": g.sync}
     SEM = {"v": "qv", "s": "qs", "t": "qt", "g": "qg"}
-    count, known, clock, hist, total = {}, {q: {} for q in Q}, {}, {}, {}
+    ops, hist, total = [], {}, {}
+    WAKE, CY, AHEAD = 130, 0.92, 140
 
     def region(v):
-        if v[0] == "ind":
-            raise ValueError("indirect")
-        if len(v) == 4:
-            return v[0], v[1], v[2], (v[3], v[1] % v[3])
-        return v[0], v[1], v[2], None
+        return v[0], v[1], v[2], (v[3], v[1] % v[3]) if len(v) == 4 else None
 
     def meets(p, q):
         if p[1] >= q[2] or q[1] >= p[2]:
@@ -64,54 +61,41 @@ def rank_program(g, core, T, topo):
     def regions(views):
         out = []
         for v in views:
-            if v is None:
-                continue
-            if v[0] == "ind":
-                out += [region(v[1]), region(v[2])]
-            else:
-                out.append(region(v))
+            out += [region(v[1]), region(v[2])] if v[0] == "ind" else [region(v)]
         return out
 
-    def prepare(q, reads, writes):
-        toks = {}
+    def add(q, kind, fn, reads, writes, dur, lat=0, sem=None, n=1, after=()):
+        me, deps = len(ops), set()
         for rs, iswrite in ((regions(reads), False), (regions(writes), True)):
             for p in rs:
-                for (h, w, tok) in hist.get(p[0], []):
+                for (h, w, o) in hist.get(p[0], []):
                     if (iswrite or w or p[0] in PSUM) and meets(p, h):
-                        toks[tok[0]] = max(toks.get(tok[0], 0), tok[1])
-        todo = [(s, n) for s, n in toks.items() if known[q].get(s, 0) < n]
-        keep = [t for t in todo if not any(o != t and clock[o].get(t[0], 0) >= t[1] for o in todo)]
-        for s, n in keep:
-            Q[q].wait_ge(T.sem[s], n)
-            for a, b in clock[(s, n)].items():
-                known[q][a] = max(known[q].get(a, 0), b)
-
-    def record(tok, q, reads, writes):
-        ck = dict(known[q]) if q else {}
-        ck[tok[0]] = tok[1]
-        clock[tok] = ck
-        total[tok[0]] = max(total.get(tok[0], 0), tok[1])
+                        deps.add(o)
+        ops.append({"q": q, "kind": kind, "fn": fn, "deps": deps, "dur": dur, "lat": lat, "sem": sem, "n": n, "after": after})
         for p in regions(writes):
             hist[p[0]] = [h for h in hist.get(p[0], []) if not (p[3] is None and p[1] <= h[0][1] and h[0][2] <= p[2])]
-            hist[p[0]].append((p, True, tok))
+            hist[p[0]].append((p, True, me))
         for p in regions(reads):
-            hist.setdefault(p[0], []).append((p, False, tok))
+            hist.setdefault(p[0], []).append((p, False, me))
+        return me
 
-    def op(q, fn, reads, writes):
-        prepare(q, reads, writes)
-        s = SEM[q]
-        count[s] = count.get(s, 0) + 1
-        fn().then_inc(T.sem[s], 1)
-        record((s, count[s]), q, reads, writes)
+    def op(q, fn, reads, writes, dur):
+        return add(q, "op", fn, reads, writes, dur)
 
-    ndma = [0]
+    ndma, loads = [0], [0]
 
-    def dma(q, out, in_, reads, writes):
-        prepare(q, reads, writes)
+    def dma(q, out, in_, reads, writes, plus=None):
+        lat = 2200 + sum([500 * width(v) // 640 for v in writes]) if not reads else 3000
+        if not reads:
+            loads[0] += lat - 2200
+            lat = 2200 + loads[0]
         s = DMASEMS[ndma[0]]
         ndma[0] += 1
-        Q[q].dma_start(out, in_).then_inc(T.sem[s], 16)
-        record((s, 16), q, reads, writes)
+        if plus:
+            fn = lambda: g.dma_start(out, in_, accum_op=A.add)
+        else:
+            fn = lambda: Q[q].dma_start(out, in_)
+        add(q, "dma", fn, reads, writes, 1000 if q == "g" else 70, lat, s, 16)
 
     def ap(v):
         if v[0] == "ind":
@@ -121,222 +105,230 @@ def rank_program(g, core, T, topo):
     def byt(v):
         return ap(v).bitcast(dt.uint8)
 
+    def width(v):
+        if v[0] == "ind":
+            return 16 * width(v[2])
+        return v[2] - v[1] if len(v) == 3 else (v[2] - v[1] + v[3] - 1) // v[3]
+
+    def cost(q, ins, two=False):
+        if ins[0][0] == "ind":
+            return 60 + width(ins[0]) * 1.5 * CY
+        n = max(width(v) for v in ins)
+        return max(64, n * (2 if two else 1)) * CY
+
     def copy(out, in_):
-        op("v", lambda: g.vector.tensor_copy(ap(out), ap(in_)), [in_], [out])
+        op("v", lambda: g.vector.tensor_copy(ap(out), ap(in_)), [in_], [out], cost("v", [in_]))
 
     def tt(out, a, b, o):
-        op("v", lambda: g.vector.tensor_tensor(ap(out), ap(a), ap(b), o), [a, b], [out])
+        two = a[0] not in PSUM and b[0] not in PSUM
+        op("v", lambda: g.vector.tensor_tensor(ap(out), ap(a), ap(b), o), [a, b], [out], cost("v", [a, b], two))
 
     def ts(out, a, s1, o1, s2=None, o2=None):
         rd = [a] + [s for s in (s1, s2) if isinstance(s, tuple)]
-        p1, p2 = [ap(s) if isinstance(s, tuple) else s for s in (s1, s2)]
-        if o2 is None:
-            op("v", lambda: g.vector.tensor_scalar(ap(out), ap(a), p1, None, o1), rd, [out])
-        else:
-            op("v", lambda: g.vector.tensor_scalar(ap(out), ap(a), p1, p2, o1, o2), rd, [out])
+
+        def fn():
+            p1, p2 = [ap(s) if isinstance(s, tuple) else s for s in (s1, s2)]
+            if o2 is None:
+                return g.vector.tensor_scalar(ap(out), ap(a), p1, None, o1)
+            return g.vector.tensor_scalar(ap(out), ap(a), p1, p2, o1, o2)
+        op("v", fn, rd, [out], cost("v", [a]))
 
     def scan(out, k, v):
-        op("v", lambda: g.vector.tensor_tensor_scan(ap(out), ap(k), ap(v), 0.0, A.add, A.max), [k, v], [out])
+        op("v", lambda: g.vector.tensor_tensor_scan(ap(out), ap(k), ap(v), 0.0, A.add, A.max), [k, v], [out], cost("v", [v]))
 
-    def act(out, in_, scale=None, bias=None):
-        if scale is None:
-            fn = lambda: g.scalar.activation(ap(out), ap(in_), F.Copy)
-        elif bias is None:
-            fn = lambda: g.scalar.activation(ap(out), ap(in_), F.Identity, scale=scale)
-        else:
-            fn = lambda: g.scalar.activation(ap(out), ap(in_), F.Identity, bias=bias, scale=scale)
-        op("s", fn, [in_], [out])
+    def act(out, in_, scale=None, bias=None, func=None):
+        rd = [in_] + ([bias] if isinstance(bias, tuple) else [])
+
+        def fn():
+            if func is not None:
+                return g.scalar.activation(ap(out), ap(in_), func, scale=scale)
+            if scale is None:
+                return g.scalar.activation(ap(out), ap(in_), F.Copy)
+            if bias is None:
+                return g.scalar.activation(ap(out), ap(in_), F.Identity, scale=scale)
+            return g.scalar.activation(ap(out), ap(in_), F.Identity, bias=ap(bias) if isinstance(bias, tuple) else bias, scale=scale)
+        op("s", fn, rd, [out], cost("s", [in_]))
 
     def quant(q, s, v):
-        op("v", lambda: g.vector.quantize_mx(ap(q), ap(s), ap(v)), [v], [q, s])
+        op("v", lambda: g.vector.quantize_mx(ap(q), ap(s), ap(v)), [v], [q, s], 12 + 0.25 * width(v))
 
     def mx(out, wq, ws, xq, xs):
-        op("t", lambda: g.tensor.matmul_mx(ap(out), ap(wq), ap(ws), ap(xq), ap(xs), True, True), [wq, ws, xq, xs], [out])
+        op("t", lambda: g.tensor.matmul_mx(ap(out), ap(wq), ap(ws), ap(xq), ap(xs), True, True), [wq, ws, xq, xs], [out], (width(xq) + 16) * CY)
 
     def iota(out, pattern, base, cm, small=False):
         if small:
             fn = lambda: g.iota(ap(out), pattern, base, cm, allow_small_or_imprecise_dtypes=True)
         else:
             fn = lambda: g.iota(ap(out), pattern, base, cm)
-        op("g", fn, [], [out])
+        op("g", fn, [], [out], 130 + 2 * width(out) * CY)
 
     def fill(out, c):
-        op("v", lambda: g.vector.memset(ap(out), c), [], [out])
+        op("v", lambda: g.vector.memset(ap(out), c), [], [out], width(out) * CY)
 
     def off4(out, s, v):
         scan(s, ("k4", 0, C), v)
         ts(out, (s[0], 3, C, 4), 4.0, A.mult, ("pc", 0, 1), A.add)
 
-    def land(buf, width, sem, n):
-        record((sem, n), None, [], [(b, 0, width) for b in buf])
-
     def send(dst, sem, out, in_, reads):
-        prepare("g", reads, [])
-        rid, pid, _ = topo.addr(dst)
-        m = topo.mask(core, dst)
-        g.remote_dma(out, in_, T.sem[sem], T.sem.rl, pid=pid, routing_id=rid, dma_engine_mask=m)
+        def fn():
+            rid, pid, _ = topo.addr(dst)
+            return g.remote_dma(out, in_, T.sem[sem], T.sem.rl, pid=pid, routing_id=rid, dma_engine_mask=topo.mask(core, dst))
         total["rl"] = total.get("rl", 0) + len(topo.engines(core, dst))
+        return add("g", "send", fn, reads, [], 900)
+
+    def land(views, sem, n, sent, lat, sent2=None, lat2=0):
+        add(None, "land", None, [], views, 0, 0, sem, n, [(sent, lat)] + ([(sent2, lat2)] if sent2 is not None else []))
 
     partner = [T.cores[rank ^ m] for m in MASKS]
-    for r in range(3):
-        e = len(topo.engines(partner[r], core))
-        land(["kp%d" % r], 20, "ak%d" % r, e)
-        land(["mq%d" % r], 40, "am%d" % r, e)
-        land(["lc%d" % r, "ls%d" % r], HALF, "ah%d" % r, 2 * e)
+    engines = [len(topo.engines(d, core)) for d in partner]
 
-    dma("y", ap(("lk", 0, 20)), T.gl[:, :], [], [("lk", 0, 20)])
-    dma("s", ap(("lk", 20, 30)), T.gk[:, 10:20], [], [("lk", 20, 30)])
-    dma("s", ap(("lk", 30, 40)), T.gk[:, 0:10], [], [("lk", 30, 40)])
+    dma("y", ap(("lk0", 0, 20)), T.gl[:, :], [], [("lk0", 0, 20)])
+    dma("s", ap(("lk0", 20, 40)), T.gk[:, :], [], [("lk0", 20, 40)])
     dma("y", ap(("ut", 0, 512)), T.u[:, :], [], [("ut", 0, 512)])
     dma("s", ap(("X", 640, 1280)), T.x[:, 640:1280], [], [("X", 640, 1280)])
     dma("y", ap(("X", 0, 640)), T.x[:, 0:640], [], [("X", 0, 640)])
-    dma("s", ap(("X2", 640, 1280)), T.x[:, 640:1280], [], [("X2", 640, 1280)])
     dma("y", byt(("wq", 0, 512)), T.wc[:, :], [], [("wq", 0, 512)])
     dma("y", ap(("wsb", 0, 512)), T.ws[:, :], [], [("wsb", 0, 512)])
     dma("y", ap(("vt", 0, 512)), T.v[:, :], [], [("vt", 0, 512)])
 
     iota(("pi", 0, 1), [[0, 1]], 0, 1)
+    iota(("ke", 0, C), [[4, C]], 131, -1)
+    iota(("it", 0, C), [[1, C]], 0, 0, True)
+    iota(("kd", 0, C), [[1, C]], 128, -1)
     iota(("ui", 0, 16), [[1, 2], [16, 8]], 0, 0)
     iota(("ci", 0, 20), [[16, 20]], 0, 0)
-    iota(("it", 0, C), [[1, C]], 0, 0, True)
-    iota(("ke", 0, C), [[4, C]], 131, -1)
-    iota(("kd", 0, C), [[1, C]], 128, -1)
+    fill(("one", 0, 512), 1.0)
     ts(("pi", 1, 2), ("pi", 0, 1), 3, A.bitwise_and)
     ts(("pi", 2, 3), ("pi", 0, 1), 12, A.bitwise_and)
     ts(("pi", 3, 4), ("pi", 0, 1), 15, A.bitwise_and)
     ts(("pc", 2, 3), ("pi", 2, 3), 1024.0, A.mult, -12288.0, A.add)
-    copy(("pc", 1, 2), ("pi", 1, 2))
-    copy(("pc", 3, 4), ("pi", 3, 4))
+    ts(("pc", 1, 2), ("pi", 1, 2), 1.0, A.mult)
+    ts(("pc", 3, 4), ("pi", 3, 4), 1.0, A.mult)
+    ts(("pc", 4, 5), ("pi", 3, 4), 16.0, A.mult, -240.0, A.add)
     tt(("pc", 0, 1), ("pc", 1, 2), ("pc", 2, 3), A.add)
-    copy(("uo", 0, 16), ("ui", 0, 16))
-    ts(("cc", 0, 20), ("ci", 0, 20), ("pc", 3, 4), A.add)
-    ts(("cc", 20, 40), ("ci", 0, 20), ("pc", 3, 4), A.add)
-    fill(("one", 0, 512), 1.0)
-
-    def lists(r):
-        n = "lko%d" % r
-        copy((n, 20, 30), ("lk", 30, 40))
-        copy((n, 30, 40), ("lk", 20, 30))
-        copy((n, 0, 20), ("lk", 0, 20))
-
-    def differences():
-        tt(("dkl", 40, 60), ("lk", 0, 20), ("cc", 0, 20), A.subtract)
-        tt(("dkl", 60, 80), ("lk", 0, 20), ("cc", 0, 20), A.subtract)
-        for a in (0, 20):
-            tt(("dkl", a, a + 10), ("lk", 30, 40), ("cc", 0, 10), A.subtract)
-            tt(("dkl", a + 10, a + 20), ("lk", 20, 30), ("cc", 10, 20), A.subtract)
-
-    def send_k(r):
-        n = "lko%d" % r
-        send(partner[r], "ak%d" % r, T["kp%d" % r][:, :], ap((n, 20, 40)), [(n, 20, 40)])
-
-    lists(0)
-    send_k(0)
-    for b in range(4):
-        op("g", lambda: g.affine_select(ap(("et", 512 * b, 512 * b + 512)), ap(("one", 0, 512)), [[-1, 512]], A.is_equal, 0.0, b, 4),
-           [("one", 0, 512)], [("et", 512 * b, 512 * b + 512)])
-    act(("lrep", 0, C), ("ind", ("it", 0, C), ("lko0", 0, 20)))
     ts(("ke", 0, C), ("ke", 0, C), 12, A.bitwise_and)
     ts(("k4", 0, C), ("ke", 0, C), 0.0, A.is_equal, -9216.0, A.mult)
     ts(("k4", 0, C), ("k4", 0, C), 1024.0, A.add)
-    off4(("l4", 0, 80), ("sl", 0, C), ("lrep", 0, C))
-    quant(("uq", 0, 128), ("us", 0, 128), ("ut", 0, 512))
-    op("v", lambda: g.vector.tensor_copy(T.up[:, 0:256].bitcast(dt.uint32), T.uq[:, 0:128].bitcast(dt.uint32).indirect(T.uo[:, 0:16])),
-       [("uq", 0, 128), ("uo", 0, 16)], [("up", 0, 256)])
-    op("s", lambda: g.scalar.activation(T.upl[:, 0:256], T.us[:, 0:128].indirect(T.uo[:, 0:16]), F.Copy),
-       [("us", 0, 128), ("uo", 0, 16)], [("upl", 0, 256)])
+    copy(("uo", 0, 16), ("ui", 0, 16))
+    ts(("kd", 0, C), ("kd", 0, C), 15, A.bitwise_and)
+    ts(("km", 0, C), ("kd", 0, C), 0.0, A.is_equal, -528.0, A.mult)
+    ts(("km", 0, C), ("km", 0, C), 16.0, A.add)
+    ts(("k16", 0, C), ("kd", 0, C), 0.0, A.is_equal, -34603008.0, A.mult)
+    ts(("k16", 0, C), ("k16", 0, C), 1048576.0, A.add)
+    fill(("base", 0, 20), 0)
+    fill(("q0", 0, 20), 1024)
+    ts(("base", 20, 40), ("ci", 0, 20), ("pc", 3, 4), A.add)
+    ts(("q0", 20, 40), ("base", 20, 40), -1.0, A.mult, 512.0, A.add)
 
-    UP, UT, US, VT = ("up", 0, 128), ("upl", 0, 128), ("up", 128, 256), ("upl", 128, 256)
+    def send_k(r):
+        n = "lko%d" % r
+        s = send(partner[r], "ak%d" % r, T["ar%d" % r][:, 0:20], ap((n, 20, 40)), [(n, 20, 40)])
+        land([("ar%d" % r, 0, 20)], "ak%d" % r, engines[r], s, 2500)
 
     def upper_signs():
         mx(("PB", 0, HALF), UP, UT, ("xq", HALF, C), ("xs", HALF, C))
+        act(("sg", 0, HALF), ("PB", 0, HALF), 1.0, func=F.Sign)
+        act(("bbK", HALF, C), ("sg", 0, HALF), 1.0, func=F.Relu)
+        act(("own", HALF, C), ("sg", 0, HALF), 4.0, func=F.Relu)
+        act(("bbL", HALF, C), ("sg", 0, HALF), 10.0, func=F.Relu)
 
-    def upper_b():
-        ts(("bb", HALF, C), ("PB", 0, HALF), 0.0, A.is_gt, 2.0, A.mult)
+    def new_lists(r):
+        n, k = "lko%d" % r, "lk%d" % r
+        copy((n, 0, 40), (k, 0, 40))
+        act(("lrep", 0, C), ("ind", ("it", 0, C), (n, 0, 20)))
+        if r < 3:
+            send_k(r)
+            off4(("l4", 0, 80), ("sl", 0, C), ("lrep", 0, C))
+            tt(("pst", 0, 40), (k, 0, 40), ("q0", 0, 40), A.add)
+            if YV:
+                act(("X2", 1280 - 320 * YV, 1280), ("X", 1280 - 320 * YV, 1280))
 
+    UP, UT, US, VT = ("up", 0, 128), ("upl", 0, 128), ("up", 128, 256), ("upl", 128, 256)
+    new_lists(0)
+    iota(("it3", 0, 1536), [[0, 3], [1, 512]], 0, 0, True)
+    quant(("uq", 0, 128), ("us", 0, 128), ("ut", 0, 512))
+    op("v", lambda: g.vector.tensor_copy(T.up[:, 0:256].bitcast(dt.uint32), T.uq[:, 0:128].bitcast(dt.uint32).indirect(T.uo[:, 0:16])),
+       [("uq", 0, 128), ("uo", 0, 16)], [("up", 0, 256)], 400)
+    op("s", lambda: g.scalar.activation(T.upl[:, 0:256], T.us[:, 0:128].indirect(T.uo[:, 0:16]), F.Copy),
+       [("us", 0, 128), ("uo", 0, 16)], [("upl", 0, 256)], 420)
     quant(("xq", HALF, C), ("xs", HALF, C), ("X", 640, 1280))
     upper_signs()
 
-    def y_piece(i):
-        a = 320 * i
-        tt(("Y", a, a + 320), ("ind", ("X", 0, 1280), ("l4", 20 * i, 20 * i + 20)), ("X2", a, a + 320), A.add)
+    def constant_tile(b):
+        op("g", lambda: g.affine_select(ap(("et", 512 * b, 512 * b + 512)), ap(("one", 0, 512)), [[-1, 512]], A.is_equal, 0.0, b, 4),
+           [("one", 0, 512)], [("et", 512 * b, 512 * b + 512)], 1150)
+
+    def bit(out, a, n):
+        ts(out, a, n, A.logical_shift_right, 1, A.bitwise_and)
 
     for r in range(3):
-        lko, m4, dst = "lko%d" % r, "m4%d" % r, partner[r]
+        lko, lk, m4, ar, dst = ["%s%d" % (a, r) for a in ("lko", "lk", "m4", "ar")] + [partner[r]]
         L, K = (lko, 0, 20), (lko, 20, 40)
         quant(("xq", 0, HALF), ("xs", 0, HALF), ("X", 0, 640))
         mx(("PA", 0, HALF), UP, UT, ("xq", 0, HALF), ("xs", 0, HALF))
         mx(("PT", 0, HALF), US, VT, ("xq", 0, HALF), ("xs", 0, HALF))
-        act(("X2", 0, 640), ("X", 0, 640))
+        for a, e in ((0, 640), (640, 1280 - 320 * YV)):
+            if a < e:
+                act(("Y", a, e), ("ind", ("X", 0, 1280), ("l4", a // 16, e // 16)))
+                dma("g", ap(("Y", a, e)), ap(("X", a, e)), [("X", a, e)], [("Y", a, e)], True)
+        for i in range(4 - YV, 4):
+            a = 320 * i
+            tt(("Y", a, a + 320), ("ind", ("X", 0, 1280), ("l4", 20 * i, 20 * i + 20)), ("X2", a, a + 320), A.add)
         if r == 0:
-            upper_b()
-        y_piece(2)
-        ts(("bb", 0, HALF), ("PA", 0, HALF), 0.0, A.is_gt, 2.0, A.mult)
-        act(("tk", 0, C), ("ind", ("bb", 0, C), K), -0.5, 2.0)
-        if r == 0:
-            ts(("kd", 0, C), ("kd", 0, C), 15, A.bitwise_and)
-            ts(("k16", 0, C), ("kd", 0, C), 0.0, A.is_equal, -135168.0, A.mult)
-            ts(("km", 0, C), ("kd", 0, C), 0.0, A.is_equal, -264.0, A.mult)
-            ts(("k16", 0, C), ("k16", 0, C), 4096.0, A.add)
-            ts(("km", 0, C), ("km", 0, C), 8.0, A.add)
-            differences()
-        else:
-            y_piece(3)
-        tt(("M", 0, C), ("ind", ("bb", 0, C), L), ("tk", 0, C), A.add)
-        act(("tk1", 0, C), ("ind", ("M", 0, C), K), 8.0)
-        y_piece(0)
+            for b in range(4):
+                constant_tile(b)
+            quant(("eq", 0, 512), ("es", 0, 512), ("et", 0, 2048))
+            quant(("vq", 0, 128), ("vs", 0, 128), ("vt", 0, 512))
+        ts(("bbK", 0, HALF), ("PA", 0, HALF), 0.0, A.is_gt)
+        ts(("own", 0, HALF), ("PA", 0, HALF), 0.0, A.is_gt, 4.0, A.mult)
+        ts(("bbL", 0, HALF), ("PA", 0, HALF), 0.0, A.is_gt, 10.0, A.mult)
+        tt(("tk", 0, C), ("ind", ("bbK", 0, C), K), ("own", 0, C), A.subtract)
+        tt(("M", 0, C), ("ind", ("bbL", 0, C), L), ("tk", 0, C), A.subtract)
+        act(("tk1", 0, C), ("ind", ("M", 0, C), K), 32.0, 66.0)
         tt(("G1", 0, C), ("ind", ("M", 0, C), L), ("tk1", 0, C), A.add)
-        act(("tk2", 0, C), ("ind", ("G1", 0, C), K), 64.0)
-        scan(("s1", 0, C), ("k16", 0, C), ("G1", 0, C))
-        scan(("sm", 0, C), ("km", 0, C), ("M", 0, C))
-        copy(("gi", 0, 20), ("s1", 15, C, 16))
-        copy(("mi", 0, 20), ("sm", 15, C, 16))
+        act(("tk2", 0, C), ("ind", ("G1", 0, C), K), 1024.0)
         tt(("G2", 0, C), ("ind", ("G1", 0, C), L), ("tk2", 0, C), A.add)
-        A0, A1, B0, B1 = [("sb", a, a + 20) for a in (40, 60, 80, 100)]
-        ts(("m7", 0, 20), ("mi", 0, 20), 7, A.bitwise_and)
-        ts(B0, ("mi", 0, 20), 1, A.bitwise_and)
-        ts(("qq", 0, 20), ("gi", 0, 20), 2, A.logical_shift_right, 1, A.bitwise_and)
-        ts(("qq", 20, 40), ("gi", 0, 20), 5, A.logical_shift_right, 1, A.bitwise_and)
-        ts(A0, ("m7", 0, 20), 3.0, A.is_ge)
-        tt(B1, ("qq", 20, 40), B0, A.not_equal)
-        tt(A1, ("qq", 0, 20), A0, A.not_equal)
+        scan(("sm", 0, C), ("km", 0, C), ("M", 0, C))
+        ts(("mi", 0, 20), ("sm", 15, C, 16), ("pc", 4, 5), A.add)
+        ts(("ab0", 0, 20), ("sm", 15, C, 16), ("pc", 4, 5), A.add, 9.0, A.is_ge)
+        ts(("ab0", 20, 40), ("mi", 0, 20), 1, A.bitwise_and)
+        tt(("u0", 0, 40), ("ab0", 0, 40), ("pst", 0, 40), A.mult)
+        ts(("sn", 0, 40), ("ab0", 0, 40), -2.0, A.mult, 1.0, A.add)
+        tt(("cs", 0, 40), ("u0", 0, 40), ("base", 0, 40), A.add)
+        tt(("ev", 0, 40), ("sn", 0, 40), ("pst", 0, 40), A.mult)
+        tt(("dm0", 0, 20), ("cs", 0, 20), ("cs", 20, 40), A.max)
+        copy(("d0", 0, 20), ("dm0", 0, 20))
+        act(("R1", 0, C), ("ind", ("it3", 0, 1536), ("d0", 0, 20)))
+        scan(("s1", 0, C), ("k16", 0, C), ("G1", 0, C))
+        copy(("gi", 0, 20), ("s1", 15, C, 16))
+        bit(("ab1", 0, 20), ("gi", 0, 20), 2)
+        bit(("ab1", 20, 40), ("gi", 0, 20), 7)
+        tt(("pr1", 0, 40), ("ab1", 0, 40), ("pst", 0, 40), A.mult)
+        tt(("cs1", 0, 40), ("pr1", 0, 40), ("base", 0, 40), A.add)
+        tt(("dm1", 0, 20), ("cs1", 0, 20), ("cs1", 20, 40), A.max)
+        ts(("da1", 0, 20), ("dm1", 0, 20), 511, A.bitwise_and)
+        copy(("d1", 0, 20), ("da1", 0, 20))
+        act(("R2", 0, C), ("ind", ("R1", 0, C), ("d1", 0, 20)))
         scan(("s2", 0, C), ("k16", 0, C), ("G2", 0, C))
-        tt(("sb", 0, 40), ("sb", 80, 120), ("sb", 40, 80), A.is_gt)
         copy(("g2", 0, 20), ("s2", 15, C, 16))
-        tt(("pr", 0, 80), ("sb", 0, 80), ("dkl", 0, 80), A.mult)
-        ts(("m2", 0, 20), ("gi", 0, 20), 7, A.bitwise_and)
-        ts(("m2", 20, 40), ("gi", 0, 20), 3, A.logical_shift_right, 7, A.bitwise_and)
-        tt(("ps", 0, 40), ("pr", 0, 40), ("pr", 40, 80), A.add)
-        ts(("by", 40, 60), ("gi", 0, 20), 1, A.bitwise_and)
-        ts(("by", 60, 80), ("gi", 0, 20), 3, A.logical_shift_right, 1, A.bitwise_and)
-        tt(("pd", 0, 40), ("ps", 0, 40), ("cc", 0, 40), A.add)
-        ts(("by", 0, 40), ("m2", 0, 40), 3.0, A.is_ge)
-        for i, s in enumerate((2, 8, 5, 11)):
-            ts(("qy", 20 * i, 20 * i + 20), ("g2", 0, 20), s, A.logical_shift_right, 1, A.bitwise_and)
-        copy(("d01", 0, 40), ("pd", 0, 40))
-        act(("R1", 0, C), ("ind", ("it", 0, C), ("d01", 0, 20)))
-        act(("R2", 0, C), ("ind", ("R1", 0, C), ("d01", 20, 40)))
-        tt(("sy", 0, 80), ("qy", 0, 80), ("by", 0, 80), A.not_equal)
-        tt(("q1", 0, 40), ("sy", 0, 40), ("sy", 40, 80), A.is_gt)
-        tt(("sb2", 20, 40), ("q1", 0, 20), A0, A.not_equal)
-        tt(("sb2", 40, 60), ("q1", 20, 40), B0, A.not_equal)
-        tt(("sb2", 0, 20), ("sb2", 40, 60), ("sb2", 20, 40), A.is_gt)
-        tt(("pr2", 0, 40), ("sb2", 0, 40), ("dkl", 20, 60), A.mult)
-        tt(("ps2", 0, 20), ("pr2", 0, 20), ("pr2", 20, 40), A.add)
-        tt(("pd2", 0, 20), ("ps2", 0, 20), ("cc", 0, 20), A.add)
-        copy(("d2", 0, 20), ("pd2", 0, 20))
-        if r == 0:
-            y_piece(3)
-        y_piece(1)
+        for i, n in enumerate((2, 12, 7, 17)):
+            bit(("qy", 20 * i, 20 * i + 20), ("g2", 0, 20), n)
+        tt(("q1", 0, 40), ("qy", 0, 40), ("qy", 40, 80), A.is_gt)
+        tt(("pr2", 0, 40), ("q1", 0, 40), ("ev", 0, 40), A.mult)
+        tt(("cs2", 0, 40), ("pr2", 0, 40), ("cs", 0, 40), A.add)
+        tt(("dm2", 0, 20), ("cs2", 0, 20), ("cs2", 20, 40), A.max)
+        ts(("da2", 0, 20), ("dm2", 0, 20), 511, A.bitwise_and)
+        copy(("d2", 0, 20), ("da2", 0, 20))
         act(("O", HALF, C), ("ind", ("R2", 0, C), ("d2", 10, 20)))
         copy(("O", 0, HALF), ("ind", ("R2", 0, C), ("d2", 0, 10)))
         off4(("o4", 0, 80), ("so", 0, C), ("O", 0, C))
-        act(("MR", 0, C), ("ind", ("O", 0, C), ("kp%d" % r, 0, 20)))
+        act(("MR", 0, C), ("ind", ("O", 0, C), (ar, 0, 20)))
         act(("Z", 640, 1280), ("ind", ("Y", 0, 1280), ("o4", 40, 80)), 0.5)
         ts(("Z", 0, 640), ("ind", ("Y", 0, 1280), ("o4", 0, 40)), 0.5, A.mult)
         quant(("zq", 0, C), ("zs", 0, C), ("Z", 0, 1280))
         off4((m4, 0, 80), ("sx", 0, C), ("MR", 0, C))
-        send(dst, "am%d" % r, T["mq%d" % r][:, :], ap((m4, 40, 80)), [(m4, 40, 80)])
+        s = send(dst, "am%d" % r, T[ar][:, 24:64], ap((m4, 40, 80)), [(m4, 40, 80)])
+        land([(ar, 24, 64)], "am%d" % r, engines[r], s, 2500)
         for b in range(4):
             mx(("P%d" % b, 0, C), ("wq", 128 * b, 128 * b + 128), ("wsb", 128 * b, 128 * b + 128), ("zq", 0, C), ("zs", 0, C))
         ts(("H", 0, 1280, 4), ("P0", 0, C), 0.03125, A.mult)
@@ -345,57 +337,105 @@ def rank_program(g, core, T, topo):
         act(("H", 3, 1280, 4), ("P3", 0, C), 0.03125)
         act(("HP", 320, 640), ("ind", ("H", 0, 1280), (m4, 20, 40)))
         copy(("HP", 0, 320), ("ind", ("H", 0, 1280), (m4, 0, 20)))
-        hq, hs = ("hq%d" % r, 0, HALF), ("hs%d" % r, 0, HALF)
+        hq, hs, lc, ls = [("%s%d" % (a, r), 0, HALF) for a in ("hq", "hs", "lc", "ls")]
         quant(hq, hs, ("HP", 0, 640))
-        send(dst, "ah%d" % r, T["lc%d" % r][:, 0:HALF].bitcast(dt.uint8), byt(hq), [hq])
-        send(dst, "ah%d" % r, T["ls%d" % r][:, 0:HALF], ap(hs), [hs])
-        tt(("X", 640, 1280), ("ind", ("H", 0, 1280), ("mq%d" % r, 0, 40)), ("X", 640, 1280), A.add)
+        s0 = send(dst, "ah%d" % r, T[lc[0]][:, 0:HALF].bitcast(dt.uint8), byt(hq), [hq])
+        s = send(dst, "ah%d" % r, T[ls[0]][:, 0:HALF], ap(hs), [hs])
+        land([lc, ls], "ah%d" % r, 2 * engines[r], s, 2600, s0, 3000)
+        tt(("X", 640, 1280), ("ind", ("H", 0, 1280), (ar, 24, 64)), ("X", 640, 1280), A.add)
         quant(("xq", HALF, C), ("xs", HALF, C), ("X", 640, 1280))
-        if r < 2:
-            act(("X2", 640, 1280), ("X", 640, 1280))
-        ts(("tu", 0, HALF), ("PT", 0, HALF), 0.0, A.is_lt)
+        act(("sgt", 0, HALF), ("PT", 0, HALF), -1.0, func=F.Sign)
+        act(("tu", 0, HALF), ("sgt", 0, HALF), 1.0, func=F.Relu)
+        tt(("xd", 0, 10), (lk, 30, 40), (lk, 0, 10), A.subtract)
+        tt(("xd", 10, 20), (lk, 20, 30), (lk, 10, 20), A.subtract)
+        scan(("st", 0, HALF), ("km", 0, HALF), ("tu", 0, HALF))
+        act(("tt", 0, 10), ("st", 15, HALF, 16), 1.0, ("pc", 4, 5))
+        act(("tt", 10, 20), ("st", 15, HALF, 16), 1.0, ("pc", 4, 5))
+        tt(("xt", 0, 20), ("tt", 0, 20), ("xd", 0, 20), A.mult)
+        n = "lk%d" % (r + 1)
+        tt((n, 0, 20), (lk, 0, 20), ("xt", 0, 20), A.add)
+        tt((n, 20, 30), (lk, 20, 30), ("xt", 10, 20), A.subtract)
+        tt((n, 30, 40), (lk, 30, 40), ("xt", 0, 10), A.subtract)
         if r < 2:
             upper_signs()
-        else:
-            quant(("vq", 0, 128), ("vs", 0, 128), ("vt", 0, 512))
+        new_lists(r + 1)
+        if r == 2:
+            act(("lrep", C, 2 * C), ("ind", ("it", 0, C), ("lko3", 20, 40)))
             mx(("PY", 0, HALF), ("vq", 0, 128), ("vs", 0, 128), ("xq", HALF, C), ("xs", HALF, C))
-        tt(("xd", 0, 20), ("lk", 20, 40), ("lk", 0, 20), A.subtract)
-        scan(("st", 0, HALF), ("km", 0, HALF), ("tu", 0, HALF))
-        if r < 2:
-            upper_b()
-        copy(("tt", 0, 10), ("st", 15, HALF, 16))
-        copy(("tt", 10, 20), ("st", 15, HALF, 16))
-        ts(("tt", 0, 20), ("tt", 0, 20), 1, A.bitwise_and)
-        tt(("xt", 0, 20), ("tt", 0, 20), ("xd", 0, 20), A.mult)
-        tt(("lk", 0, 20), ("lk", 0, 20), ("xt", 0, 20), A.add)
-        tt(("lk", 20, 40), ("lk", 20, 40), ("xt", 0, 20), A.subtract)
-        lists(r + 1)
-        n = "lko%d" % (r + 1)
-        act(("lrep", 0, C), ("ind", ("it", 0, C), (n, 0, 20)))
-        if r < 2:
-            send_k(r + 1)
-            differences()
-            off4(("l4", 0, 80), ("sl", 0, C), ("lrep", 0, C))
-        else:
-            act(("lrep", C, 2 * C), ("ind", ("it", 0, C), (n, 20, 40)))
             act(("ysb", HALF, C), ("PY", 0, HALF))
             dma("y", T.y[:, HALF:C], ap(("ysb", HALF, C)), [("ysb", HALF, C)], [])
             dma("y", T.oc[:, 4 * HALF:4 * C], byt(("xq", HALF, C)), [("xq", HALF, C)], [])
             for k in range(4):
                 dma("y", T.osc[4 * k:4 * k + 4, HALF:C], T.xs[32 * k:32 * k + 4, HALF:C], [("xs", HALF, C)], [])
             dma("y", T.lr[:, :], T.lrep[::16, :], [("lrep", 0, 2 * C)], [])
-        if r == 0:
-            quant(("eq", 0, 512), ("es", 0, 512), ("et", 0, 2048))
         for b in range(4):
-            mx(("P%d" % b, 0, HALF), ("eq", 128 * b, 128 * b + 128), ("es", 128 * b, 128 * b + 128), ("lc%d" % r, 0, HALF), ("ls%d" % r, 0, HALF))
+            mx(("P%d" % b, 0, HALF), ("eq", 128 * b, 128 * b + 128), ("es", 128 * b, 128 * b + 128), lc, ls)
         for b in range(4):
             tt(("X", b, 640, 4), ("P%d" % b, 0, HALF), ("X", b, 640, 4), A.add)
     quant(("xq", 0, HALF), ("xs", 0, HALF), ("X", 0, 640))
     mx(("PA", 0, HALF), ("vq", 0, 128), ("vs", 0, 128), ("xq", 0, HALF), ("xs", 0, HALF))
-    dma("y", T.oc[:, 0:4 * HALF], byt(("xq", 0, HALF)), [("xq", 0, HALF)], [])
-    for k in range(4):
-        dma("y" if k % 2 else "s", T.osc[4 * k:4 * k + 4, 0:HALF], T.xs[32 * k:32 * k + 4, 0:HALF], [("xs", 0, HALF)], [])
     copy(("ysb", 0, HALF), ("PA", 0, HALF))
     dma("y", T.y[:, 0:HALF], ap(("ysb", 0, HALF)), [("ysb", 0, HALF)], [])
+    dma("y", T.oc[:, 0:4 * HALF], byt(("xq", 0, HALF)), [("xq", 0, HALF)], [])
+    for k in range(4):
+        dma("s" if k % 2 else "y", T.osc[4 * k:4 * k + 4, 0:HALF], T.xs[32 * k:32 * k + 4, 0:HALF], [("xs", 0, HALF)], [])
+
+    n = len(ops)
+    users = [[] for _ in range(n)]
+    for i, o in enumerate(ops):
+        for d in o["deps"]:
+            users[d].append(i)
+        for d, _ in o["after"]:
+            users[d].append(i)
+    way = [0.0] * n
+    for i in range(n - 1, -1, -1):
+        way[i] = ops[i]["dur"] + ops[i]["lat"] + max([way[u] + WAKE + dict(ops[u]["after"]).get(i, 0) for u in users[i]], default=0)
+    left = [len(o["deps"]) + len(o["after"]) for o in ops]
+    early, free, end = [0.0] * n, {q: 0.0 for q in Q}, [0.0] * n
+    ready, order = [i for i in range(n) if left[i] == 0], []
+    while ready:
+        est = {i: max(early[i], free[ops[i]["q"]]) if ops[i]["q"] else early[i] for i in ready}
+        first = min(est.values())
+        i = max([j for j in ready if est[j] <= first + AHEAD], key=lambda j: (way[j], -j))
+        fits = [j for j in ready if ops[j]["q"] == ops[i]["q"] and j != i and est[j] + ops[j]["dur"] <= est[i] + 20]
+        if fits and ops[i]["q"]:
+            i = max(fits, key=lambda j: (way[j], -j))
+        ready.remove(i)
+        order.append((est[i], len(order), i))
+        if ops[i]["q"]:
+            free[ops[i]["q"]] = est[i] + ops[i]["dur"]
+        end[i] = est[i] + ops[i]["dur"] + ops[i]["lat"]
+        for u in users[i]:
+            left[u] -= 1
+            early[u] = max(early[u], end[i] + WAKE + dict(ops[u]["after"]).get(i, 0))
+            if left[u] == 0:
+                ready.append(u)
+
+    count, known, clock, token = {}, {q: {} for q in Q}, {}, {}
+    for _, _, i in order:
+        o, q = ops[i], ops[i]["q"]
+        if o["kind"] == "land":
+            token[i] = (o["sem"], o["n"])
+            clock[token[i]] = {o["sem"]: o["n"]}
+            total[o["sem"]] = o["n"]
+            continue
+        toks = {}
+        for d in o["deps"]:
+            if d in token:
+                toks[token[d][0]] = max(toks.get(token[d][0], 0), token[d][1])
+        todo = [t for t in toks.items() if known[q].get(t[0], 0) < t[1]]
+        for t in sorted(t for t in todo if not any(u != t and clock[u].get(t[0], 0) >= t[1] for u in todo)):
+            Q[q].wait_ge(T.sem[t[0]], t[1])
+            for a, b in clock[t].items():
+                known[q][a] = max(known[q].get(a, 0), b)
+        ins = o["fn"]()
+        if o["kind"] == "send":
+            continue
+        s = o["sem"] or SEM[q]
+        count[s] = total[s] = count.get(s, 0) + o["n"]
+        ins.then_inc(T.sem[s], o["n"])
+        token[i] = (s, count[s])
+        clock[token[i]] = dict(known[q])
+        clock[token[i]][s] = count[s]
     for s in sorted(total):
         g.wait_ge(T.sem[s], total[s])

from concourse.mybir import dt, AluOpType, ActivationFunctionType

MASKS = [1, 2, 4]
C, HALF = 320, 160
YV = 0
CODES, U8, BF, F32, I32, U16 = "float8_e4m3fn_x4", "uint8", "bfloat16", "float32", "int32", "uint16"
SCRATCH = {}
for _n, _w, _d in [
    ("X", 1280, BF), ("X2", 1280, BF), ("Y", 1280, BF), ("Z", 1280, BF), ("H", 1280, BF), ("HP", 640, BF),
    ("xq", 320, CODES), ("xs", 320, U8), ("zq", 320, CODES), ("zs", 320, U8),
    ("ut", 512, BF), ("uq", 128, CODES), ("us", 128, U8), ("up", 256, CODES), ("upl", 256, U8), ("uo", 16, U16), ("ui", 16, I32),
    ("vt", 512, BF), ("vq", 128, CODES), ("vs", 128, U8), ("wq", 512, CODES), ("wsb", 512, U8),
    ("et", 2048, BF), ("eq", 512, CODES), ("es", 512, U8), ("one", 512, BF),
    ("it", 320, F32), ("it3", 1536, F32), ("kd", 320, I32), ("ke", 320, I32), ("km", 320, BF), ("k16", 320, F32), ("k4", 320, F32),
    ("pi", 8, I32), ("pc", 8, F32), ("ci", 20, I32), ("base", 40, I32), ("q0", 40, I32), ("pst", 40, I32),
    ("l4", 80, U16), ("bbK", 320, BF), ("bbL", 320, BF), ("own", 320, BF), ("tk", 320, BF), ("M", 320, BF),
    ("tk1", 320, F32), ("G1", 320, F32), ("tk2", 320, F32), ("G2", 320, F32),
    ("sm", 320, BF), ("s1", 320, F32), ("s2", 320, F32), ("so", 320, F32), ("sx", 320, F32), ("sl", 320, F32),
    ("mi", 20, I32), ("gi", 20, I32), ("g2", 20, I32), ("qy", 80, I32), ("q1", 40, I32), ("ab0", 40, I32), ("ab1", 40, I32),
    ("u0", 40, I32), ("cs", 40, I32), ("sn", 40, I32), ("ev", 40, I32), ("pr1", 40, I32), ("cs1", 40, I32), ("pr2", 40, I32), ("cs2", 40, I32),
    ("dm0", 20, I32), ("dm1", 20, I32), ("da1", 20, I32), ("dm2", 20, I32), ("da2", 20, I32), ("d0", 20, U16), ("d1", 20, U16), ("d2", 20, U16),
    ("sg", 160, BF), ("sgt", 160, BF), ("R1", 320, F32), ("R2", 320, F32), ("O", 320, F32), ("o4", 80, U16), ("MR", 320, F32),
    ("lrep", 640, F32), ("tu", 160, BF), ("st", 160, BF), ("tt", 20, F32), ("xd", 20, I32), ("xt", 20, I32), ("ysb", 320, F32),
]:
    SCRATCH[_n] = ("sbuf", [128, _w], _d)
for _r in range(3):
    SCRATCH["hq%d" % _r] = ("sbuf", [128, HALF], CODES)
    SCRATCH["hs%d" % _r] = ("sbuf", [128, HALF], U8)
    SCRATCH["lc%d" % _r] = ("sbuf", [128, HALF], CODES)
    SCRATCH["ls%d" % _r] = ("sbuf", [128, HALF], U8)
    SCRATCH["ar%d" % _r] = ("sbuf", [128, 64], U16)
    SCRATCH["m4%d" % _r] = ("sbuf", [128, 80], U16)
for _r in range(4):
    SCRATCH["lko%d" % _r] = ("sbuf", [128, 40], U16)
    SCRATCH["lk%d" % _r] = ("sbuf", [128, 40], I32)
PSUM = ["PA", "PB", "PT", "PY", "P0", "P1", "P2", "P3"]
for _n in PSUM:
    SCRATCH[_n] = ("psum", [128, 512], F32)
DMASEMS = ["dm%d" % i for i in range(40)]
SEMAPHORES = ["qv", "qs", "qt", "qg", "rl"] + [a + str(r) for a in ("ak", "am", "ah") for r in range(3)] + DMASEMS


def rank_program(g, core, T, topo):
    rank = T.rank_of(core)
    if rank is None:
        return
    A, F = AluOpType, ActivationFunctionType
    Q = {"v": g.vector, "s": g.scalar, "t": g.tensor, "g": g, "y": g.sync}
    SEM = {"v": "qv", "s": "qs", "t": "qt", "g": "qg"}
    ops, hist, total = [], {}, {}
    WAKE, CY, AHEAD = 130, 0.92, 140

    def region(v):
        return v[0], v[1], v[2], (v[3], v[1] % v[3]) if len(v) == 4 else None

    def meets(p, q):
        if p[1] >= q[2] or q[1] >= p[2]:
            return False
        return not (p[3] and q[3] and p[3][0] == q[3][0] and p[3][1] != q[3][1])

    def regions(views):
        out = []
        for v in views:
            out += [region(v[1]), region(v[2])] if v[0] == "ind" else [region(v)]
        return out

    def add(q, kind, fn, reads, writes, dur, lat=0, sem=None, n=1, after=()):
        me, deps = len(ops), set()
        for rs, iswrite in ((regions(reads), False), (regions(writes), True)):
            for p in rs:
                for (h, w, o) in hist.get(p[0], []):
                    if (iswrite or w or p[0] in PSUM) and meets(p, h):
                        deps.add(o)
        ops.append({"q": q, "kind": kind, "fn": fn, "deps": deps, "dur": dur, "lat": lat, "sem": sem, "n": n, "after": after})
        for p in regions(writes):
            hist[p[0]] = [h for h in hist.get(p[0], []) if not (p[3] is None and p[1] <= h[0][1] and h[0][2] <= p[2])]
            hist[p[0]].append((p, True, me))
        for p in regions(reads):
            hist.setdefault(p[0], []).append((p, False, me))
        return me

    def op(q, fn, reads, writes, dur):
        return add(q, "op", fn, reads, writes, dur)

    ndma, loads = [0], [0]

    def dma(q, out, in_, reads, writes, plus=None):
        lat = 2200 + sum([500 * width(v) // 640 for v in writes]) if not reads else 3000
        if not reads:
            loads[0] += lat - 2200
            lat = 2200 + loads[0]
        s = DMASEMS[ndma[0]]
        ndma[0] += 1
        if plus:
            fn = lambda: g.dma_start(out, in_, accum_op=A.add)
        else:
            fn = lambda: Q[q].dma_start(out, in_)
        add(q, "dma", fn, reads, writes, 1000 if q == "g" else 70, lat, s, 16)

    def ap(v):
        if v[0] == "ind":
            return ap(v[1]).indirect(ap(v[2]))
        return T[v[0]][:, v[1]:v[2]] if len(v) == 3 else T[v[0]][:, v[1]:v[2]:v[3]]

    def byt(v):
        return ap(v).bitcast(dt.uint8)

    def width(v):
        if v[0] == "ind":
            return 16 * width(v[2])
        return v[2] - v[1] if len(v) == 3 else (v[2] - v[1] + v[3] - 1) // v[3]

    def cost(q, ins, two=False):
        if ins[0][0] == "ind":
            return 60 + width(ins[0]) * 1.5 * CY
        n = max(width(v) for v in ins)
        return max(64, n * (2 if two else 1)) * CY

    def copy(out, in_):
        op("v", lambda: g.vector.tensor_copy(ap(out), ap(in_)), [in_], [out], cost("v", [in_]))

    def tt(out, a, b, o):
        two = a[0] not in PSUM and b[0] not in PSUM
        op("v", lambda: g.vector.tensor_tensor(ap(out), ap(a), ap(b), o), [a, b], [out], cost("v", [a, b], two))

    def ts(out, a, s1, o1, s2=None, o2=None):
        rd = [a] + [s for s in (s1, s2) if isinstance(s, tuple)]

        def fn():
            p1, p2 = [ap(s) if isinstance(s, tuple) else s for s in (s1, s2)]
            if o2 is None:
                return g.vector.tensor_scalar(ap(out), ap(a), p1, None, o1)
            return g.vector.tensor_scalar(ap(out), ap(a), p1, p2, o1, o2)
        op("v", fn, rd, [out], cost("v", [a]))

    def scan(out, k, v):
        op("v", lambda: g.vector.tensor_tensor_scan(ap(out), ap(k), ap(v), 0.0, A.add, A.max), [k, v], [out], cost("v", [v]))

    def act(out, in_, scale=None, bias=None, func=None):
        rd = [in_] + ([bias] if isinstance(bias, tuple) else [])

        def fn():
            if func is not None:
                return g.scalar.activation(ap(out), ap(in_), func, scale=scale)
            if scale is None:
                return g.scalar.activation(ap(out), ap(in_), F.Copy)
            if bias is None:
                return g.scalar.activation(ap(out), ap(in_), F.Identity, scale=scale)
            return g.scalar.activation(ap(out), ap(in_), F.Identity, bias=ap(bias) if isinstance(bias, tuple) else bias, scale=scale)
        op("s", fn, rd, [out], cost("s", [in_]))

    def quant(q, s, v):
        op("v", lambda: g.vector.quantize_mx(ap(q), ap(s), ap(v)), [v], [q, s], 12 + 0.25 * width(v))

    def mx(out, wq, ws, xq, xs):
        op("t", lambda: g.tensor.matmul_mx(ap(out), ap(wq), ap(ws), ap(xq), ap(xs), True, True), [wq, ws, xq, xs], [out], (width(xq) + 16) * CY)

    def iota(out, pattern, base, cm, small=False):
        if small:
            fn = lambda: g.iota(ap(out), pattern, base, cm, allow_small_or_imprecise_dtypes=True)
        else:
            fn = lambda: g.iota(ap(out), pattern, base, cm)
        op("g", fn, [], [out], 130 + 2 * width(out) * CY)

    def fill(out, c):
        op("v", lambda: g.vector.memset(ap(out), c), [], [out], width(out) * CY)

    def off4(out, s, v):
        scan(s, ("k4", 0, C), v)
        ts(out, (s[0], 3, C, 4), 4.0, A.mult, ("pc", 0, 1), A.add)

    def send(dst, sem, out, in_, reads):
        def fn():
            rid, pid, _ = topo.addr(dst)
            return g.remote_dma(out, in_, T.sem[sem], T.sem.rl, pid=pid, routing_id=rid, dma_engine_mask=topo.mask(core, dst))
        total["rl"] = total.get("rl", 0) + len(topo.engines(core, dst))
        return add("g", "send", fn, reads, [], 900)

    def land(views, sem, n, sent, lat, sent2=None, lat2=0):
        add(None, "land", None, [], views, 0, 0, sem, n, [(sent, lat)] + ([(sent2, lat2)] if sent2 is not None else []))

    partner = [T.cores[rank ^ m] for m in MASKS]
    engines = [len(topo.engines(d, core)) for d in partner]

    dma("y", ap(("lk0", 0, 20)), T.gl[:, :], [], [("lk0", 0, 20)])
    dma("s", ap(("lk0", 20, 40)), T.gk[:, :], [], [("lk0", 20, 40)])
    dma("y", ap(("ut", 0, 512)), T.u[:, :], [], [("ut", 0, 512)])
    dma("s", ap(("X", 640, 1280)), T.x[:, 640:1280], [], [("X", 640, 1280)])
    dma("y", ap(("X", 0, 640)), T.x[:, 0:640], [], [("X", 0, 640)])
    dma("y", byt(("wq", 0, 512)), T.wc[:, :], [], [("wq", 0, 512)])
    dma("y", ap(("wsb", 0, 512)), T.ws[:, :], [], [("wsb", 0, 512)])
    dma("y", ap(("vt", 0, 512)), T.v[:, :], [], [("vt", 0, 512)])

    iota(("pi", 0, 1), [[0, 1]], 0, 1)
    iota(("ke", 0, C), [[4, C]], 131, -1)
    iota(("it", 0, C), [[1, C]], 0, 0, True)
    iota(("kd", 0, C), [[1, C]], 128, -1)
    iota(("ui", 0, 16), [[1, 2], [16, 8]], 0, 0)
    iota(("ci", 0, 20), [[16, 20]], 0, 0)
    fill(("one", 0, 512), 1.0)
    ts(("pi", 1, 2), ("pi", 0, 1), 3, A.bitwise_and)
    ts(("pi", 2, 3), ("pi", 0, 1), 12, A.bitwise_and)
    ts(("pi", 3, 4), ("pi", 0, 1), 15, A.bitwise_and)
    ts(("pc", 2, 3), ("pi", 2, 3), 1024.0, A.mult, -12288.0, A.add)
    ts(("pc", 1, 2), ("pi", 1, 2), 1.0, A.mult)
    ts(("pc", 3, 4), ("pi", 3, 4), 1.0, A.mult)
    ts(("pc", 4, 5), ("pi", 3, 4), 16.0, A.mult, -240.0, A.add)
    tt(("pc", 0, 1), ("pc", 1, 2), ("pc", 2, 3), A.add)
    ts(("ke", 0, C), ("ke", 0, C), 12, A.bitwise_and)
    ts(("k4", 0, C), ("ke", 0, C), 0.0, A.is_equal, -9216.0, A.mult)
    ts(("k4", 0, C), ("k4", 0, C), 1024.0, A.add)
    copy(("uo", 0, 16), ("ui", 0, 16))
    ts(("kd", 0, C), ("kd", 0, C), 15, A.bitwise_and)
    ts(("km", 0, C), ("kd", 0, C), 0.0, A.is_equal, -528.0, A.mult)
    ts(("km", 0, C), ("km", 0, C), 16.0, A.add)
    ts(("k16", 0, C), ("kd", 0, C), 0.0, A.is_equal, -34603008.0, A.mult)
    ts(("k16", 0, C), ("k16", 0, C), 1048576.0, A.add)
    fill(("base", 0, 20), 0)
    fill(("q0", 0, 20), 1024)
    ts(("base", 20, 40), ("ci", 0, 20), ("pc", 3, 4), A.add)
    ts(("q0", 20, 40), ("base", 20, 40), -1.0, A.mult, 512.0, A.add)

    def send_k(r):
        n = "lko%d" % r
        s = send(partner[r], "ak%d" % r, T["ar%d" % r][:, 0:20], ap((n, 20, 40)), [(n, 20, 40)])
        land([("ar%d" % r, 0, 20)], "ak%d" % r, engines[r], s, 2500)

    def upper_signs():
        mx(("PB", 0, HALF), UP, UT, ("xq", HALF, C), ("xs", HALF, C))
        act(("sg", 0, HALF), ("PB", 0, HALF), 1.0, func=F.Sign)
        act(("bbK", HALF, C), ("sg", 0, HALF), 1.0, func=F.Relu)
        act(("own", HALF, C), ("sg", 0, HALF), 4.0, func=F.Relu)
        act(("bbL", HALF, C), ("sg", 0, HALF), 10.0, func=F.Relu)

    def new_lists(r):
        n, k = "lko%d" % r, "lk%d" % r
        copy((n, 0, 40), (k, 0, 40))
        act(("lrep", 0, C), ("ind", ("it", 0, C), (n, 0, 20)))
        if r < 3:
            send_k(r)
            off4(("l4", 0, 80), ("sl", 0, C), ("lrep", 0, C))
            tt(("pst", 0, 40), (k, 0, 40), ("q0", 0, 40), A.add)
            if YV:
                act(("X2", 1280 - 320 * YV, 1280), ("X", 1280 - 320 * YV, 1280))

    UP, UT, US, VT = ("up", 0, 128), ("upl", 0, 128), ("up", 128, 256), ("upl", 128, 256)
    new_lists(0)
    iota(("it3", 0, 1536), [[0, 3], [1, 512]], 0, 0, True)
    quant(("uq", 0, 128), ("us", 0, 128), ("ut", 0, 512))
    op("v", lambda: g.vector.tensor_copy(T.up[:, 0:256].bitcast(dt.uint32), T.uq[:, 0:128].bitcast(dt.uint32).indirect(T.uo[:, 0:16])),
       [("uq", 0, 128), ("uo", 0, 16)], [("up", 0, 256)], 400)
    op("s", lambda: g.scalar.activation(T.upl[:, 0:256], T.us[:, 0:128].indirect(T.uo[:, 0:16]), F.Copy),
       [("us", 0, 128), ("uo", 0, 16)], [("upl", 0, 256)], 420)
    quant(("xq", HALF, C), ("xs", HALF, C), ("X", 640, 1280))
    upper_signs()

    def constant_tile(b):
        op("g", lambda: g.affine_select(ap(("et", 512 * b, 512 * b + 512)), ap(("one", 0, 512)), [[-1, 512]], A.is_equal, 0.0, b, 4),
           [("one", 0, 512)], [("et", 512 * b, 512 * b + 512)], 1150)

    def bit(out, a, n):
        ts(out, a, n, A.logical_shift_right, 1, A.bitwise_and)

    for r in range(3):
        lko, lk, m4, ar, dst = ["%s%d" % (a, r) for a in ("lko", "lk", "m4", "ar")] + [partner[r]]
        L, K = (lko, 0, 20), (lko, 20, 40)
        quant(("xq", 0, HALF), ("xs", 0, HALF), ("X", 0, 640))
        mx(("PA", 0, HALF), UP, UT, ("xq", 0, HALF), ("xs", 0, HALF))
        mx(("PT", 0, HALF), US, VT, ("xq", 0, HALF), ("xs", 0, HALF))
        for a, e in ((0, 640), (640, 1280 - 320 * YV)):
            if a < e:
                act(("Y", a, e), ("ind", ("X", 0, 1280), ("l4", a // 16, e // 16)))
                dma("g", ap(("Y", a, e)), ap(("X", a, e)), [("X", a, e)], [("Y", a, e)], True)
        for i in range(4 - YV, 4):
            a = 320 * i
            tt(("Y", a, a + 320), ("ind", ("X", 0, 1280), ("l4", 20 * i, 20 * i + 20)), ("X2", a, a + 320), A.add)
        if r == 0:
            for b in range(4):
                constant_tile(b)
            quant(("eq", 0, 512), ("es", 0, 512), ("et", 0, 2048))
            quant(("vq", 0, 128), ("vs", 0, 128), ("vt", 0, 512))
        ts(("bbK", 0, HALF), ("PA", 0, HALF), 0.0, A.is_gt)
        ts(("own", 0, HALF), ("PA", 0, HALF), 0.0, A.is_gt, 4.0, A.mult)
        ts(("bbL", 0, HALF), ("PA", 0, HALF), 0.0, A.is_gt, 10.0, A.mult)
        tt(("tk", 0, C), ("ind", ("bbK", 0, C), K), ("own", 0, C), A.subtract)
        tt(("M", 0, C), ("ind", ("bbL", 0, C), L), ("tk", 0, C), A.subtract)
        act(("tk1", 0, C), ("ind", ("M", 0, C), K), 32.0, 66.0)
        tt(("G1", 0, C), ("ind", ("M", 0, C), L), ("tk1", 0, C), A.add)
        act(("tk2", 0, C), ("ind", ("G1", 0, C), K), 1024.0)
        tt(("G2", 0, C), ("ind", ("G1", 0, C), L), ("tk2", 0, C), A.add)
        scan(("sm", 0, C), ("km", 0, C), ("M", 0, C))
        ts(("mi", 0, 20), ("sm", 15, C, 16), ("pc", 4, 5), A.add)
        ts(("ab0", 0, 20), ("sm", 15, C, 16), ("pc", 4, 5), A.add, 9.0, A.is_ge)
        ts(("ab0", 20, 40), ("mi", 0, 20), 1, A.bitwise_and)
        tt(("u0", 0, 40), ("ab0", 0, 40), ("pst", 0, 40), A.mult)
        ts(("sn", 0, 40), ("ab0", 0, 40), -2.0, A.mult, 1.0, A.add)
        tt(("cs", 0, 40), ("u0", 0, 40), ("base", 0, 40), A.add)
        tt(("ev", 0, 40), ("sn", 0, 40), ("pst", 0, 40), A.mult)
        tt(("dm0", 0, 20), ("cs", 0, 20), ("cs", 20, 40), A.max)
        copy(("d0", 0, 20), ("dm0", 0, 20))
        act(("R1", 0, C), ("ind", ("it3", 0, 1536), ("d0", 0, 20)))
        scan(("s1", 0, C), ("k16", 0, C), ("G1", 0, C))
        copy(("gi", 0, 20), ("s1", 15, C, 16))
        bit(("ab1", 0, 20), ("gi", 0, 20), 2)
        bit(("ab1", 20, 40), ("gi", 0, 20), 7)
        tt(("pr1", 0, 40), ("ab1", 0, 40), ("pst", 0, 40), A.mult)
        tt(("cs1", 0, 40), ("pr1", 0, 40), ("base", 0, 40), A.add)
        tt(("dm1", 0, 20), ("cs1", 0, 20), ("cs1", 20, 40), A.max)
        ts(("da1", 0, 20), ("dm1", 0, 20), 511, A.bitwise_and)
        copy(("d1", 0, 20), ("da1", 0, 20))
        act(("R2", 0, C), ("ind", ("R1", 0, C), ("d1", 0, 20)))
        scan(("s2", 0, C), ("k16", 0, C), ("G2", 0, C))
        copy(("g2", 0, 20), ("s2", 15, C, 16))
        for i, n in enumerate((2, 12, 7, 17)):
            bit(("qy", 20 * i, 20 * i + 20), ("g2", 0, 20), n)
        tt(("q1", 0, 40), ("qy", 0, 40), ("qy", 40, 80), A.is_gt)
        tt(("pr2", 0, 40), ("q1", 0, 40), ("ev", 0, 40), A.mult)
        tt(("cs2", 0, 40), ("pr2", 0, 40), ("cs", 0, 40), A.add)
        tt(("dm2", 0, 20), ("cs2", 0, 20), ("cs2", 20, 40), A.max)
        ts(("da2", 0, 20), ("dm2", 0, 20), 511, A.bitwise_and)
        copy(("d2", 0, 20), ("da2", 0, 20))
        act(("O", HALF, C), ("ind", ("R2", 0, C), ("d2", 10, 20)))
        copy(("O", 0, HALF), ("ind", ("R2", 0, C), ("d2", 0, 10)))
        off4(("o4", 0, 80), ("so", 0, C), ("O", 0, C))
        act(("MR", 0, C), ("ind", ("O", 0, C), (ar, 0, 20)))
        act(("Z", 640, 1280), ("ind", ("Y", 0, 1280), ("o4", 40, 80)), 0.5)
        ts(("Z", 0, 640), ("ind", ("Y", 0, 1280), ("o4", 0, 40)), 0.5, A.mult)
        quant(("zq", 0, C), ("zs", 0, C), ("Z", 0, 1280))
        off4((m4, 0, 80), ("sx", 0, C), ("MR", 0, C))
        s = send(dst, "am%d" % r, T[ar][:, 24:64], ap((m4, 40, 80)), [(m4, 40, 80)])
        land([(ar, 24, 64)], "am%d" % r, engines[r], s, 2500)
        for b in range(4):
            mx(("P%d" % b, 0, C), ("wq", 128 * b, 128 * b + 128), ("wsb", 128 * b, 128 * b + 128), ("zq", 0, C), ("zs", 0, C))
        ts(("H", 0, 1280, 4), ("P0", 0, C), 0.03125, A.mult)
        act(("H", 1, 1280, 4), ("P1", 0, C), 0.03125)
        ts(("H", 2, 1280, 4), ("P2", 0, C), 0.03125, A.mult)
        act(("H", 3, 1280, 4), ("P3", 0, C), 0.03125)
        act(("HP", 320, 640), ("ind", ("H", 0, 1280), (m4, 20, 40)))
        copy(("HP", 0, 320), ("ind", ("H", 0, 1280), (m4, 0, 20)))
        hq, hs, lc, ls = [("%s%d" % (a, r), 0, HALF) for a in ("hq", "hs", "lc", "ls")]
        quant(hq, hs, ("HP", 0, 640))
        s0 = send(dst, "ah%d" % r, T[lc[0]][:, 0:HALF].bitcast(dt.uint8), byt(hq), [hq])
        s = send(dst, "ah%d" % r, T[ls[0]][:, 0:HALF], ap(hs), [hs])
        land([lc, ls], "ah%d" % r, 2 * engines[r], s, 2600, s0, 3000)
        tt(("X", 640, 1280), ("ind", ("H", 0, 1280), (ar, 24, 64)), ("X", 640, 1280), A.add)
        quant(("xq", HALF, C), ("xs", HALF, C), ("X", 640, 1280))
        act(("sgt", 0, HALF), ("PT", 0, HALF), -1.0, func=F.Sign)
        act(("tu", 0, HALF), ("sgt", 0, HALF), 1.0, func=F.Relu)
        tt(("xd", 0, 10), (lk, 30, 40), (lk, 0, 10), A.subtract)
        tt(("xd", 10, 20), (lk, 20, 30), (lk, 10, 20), A.subtract)
        scan(("st", 0, HALF), ("km", 0, HALF), ("tu", 0, HALF))
        act(("tt", 0, 10), ("st", 15, HALF, 16), 1.0, ("pc", 4, 5))
        act(("tt", 10, 20), ("st", 15, HALF, 16), 1.0, ("pc", 4, 5))
        tt(("xt", 0, 20), ("tt", 0, 20), ("xd", 0, 20), A.mult)
        n = "lk%d" % (r + 1)
        tt((n, 0, 20), (lk, 0, 20), ("xt", 0, 20), A.add)
        tt((n, 20, 30), (lk, 20, 30), ("xt", 10, 20), A.subtract)
        tt((n, 30, 40), (lk, 30, 40), ("xt", 0, 10), A.subtract)
        if r < 2:
            upper_signs()
        new_lists(r + 1)
        if r == 2:
            act(("lrep", C, 2 * C), ("ind", ("it", 0, C), ("lko3", 20, 40)))
            mx(("PY", 0, HALF), ("vq", 0, 128), ("vs", 0, 128), ("xq", HALF, C), ("xs", HALF, C))
            act(("ysb", HALF, C), ("PY", 0, HALF))
            dma("y", T.y[:, HALF:C], ap(("ysb", HALF, C)), [("ysb", HALF, C)], [])
            dma("y", T.oc[:, 4 * HALF:4 * C], byt(("xq", HALF, C)), [("xq", HALF, C)], [])
            for k in range(4):
                dma("y", T.osc[4 * k:4 * k + 4, HALF:C], T.xs[32 * k:32 * k + 4, HALF:C], [("xs", HALF, C)], [])
            dma("y", T.lr[:, :], T.lrep[::16, :], [("lrep", 0, 2 * C)], [])
        for b in range(4):
            mx(("P%d" % b, 0, HALF), ("eq", 128 * b, 128 * b + 128), ("es", 128 * b, 128 * b + 128), lc, ls)
        for b in range(4):
            tt(("X", b, 640, 4), ("P%d" % b, 0, HALF), ("X", b, 640, 4), A.add)
    quant(("xq", 0, HALF), ("xs", 0, HALF), ("X", 0, 640))
    mx(("PA", 0, HALF), ("vq", 0, 128), ("vs", 0, 128), ("xq", 0, HALF), ("xs", 0, HALF))
    copy(("ysb", 0, HALF), ("PA", 0, HALF))
    dma("y", T.y[:, 0:HALF], ap(("ysb", 0, HALF)), [("ysb", 0, HALF)], [])
    dma("y", T.oc[:, 0:4 * HALF], byt(("xq", 0, HALF)), [("xq", 0, HALF)], [])
    for k in range(4):
        dma("s" if k % 2 else "y", T.osc[4 * k:4 * k + 4, 0:HALF], T.xs[32 * k:32 * k + 4, 0:HALF], [("xs", 0, HALF)], [])

    n = len(ops)
    users = [[] for _ in range(n)]
    for i, o in enumerate(ops):
        for d in o["deps"]:
            users[d].append(i)
        for d, _ in o["after"]:
            users[d].append(i)
    way = [0.0] * n
    for i in range(n - 1, -1, -1):
        way[i] = ops[i]["dur"] + ops[i]["lat"] + max([way[u] + WAKE + dict(ops[u]["after"]).get(i, 0) for u in users[i]], default=0)
    left = [len(o["deps"]) + len(o["after"]) for o in ops]
    early, free, end = [0.0] * n, {q: 0.0 for q in Q}, [0.0] * n
    ready, order = [i for i in range(n) if left[i] == 0], []
    while ready:
        est = {i: max(early[i], free[ops[i]["q"]]) if ops[i]["q"] else early[i] for i in ready}
        first = min(est.values())
        i = max([j for j in ready if est[j] <= first + AHEAD], key=lambda j: (way[j], -j))
        fits = [j for j in ready if ops[j]["q"] == ops[i]["q"] and j != i and est[j] + ops[j]["dur"] <= est[i] + 20]
        if fits and ops[i]["q"]:
            i = max(fits, key=lambda j: (way[j], -j))
        ready.remove(i)
        order.append((est[i], len(order), i))
        if ops[i]["q"]:
            free[ops[i]["q"]] = est[i] + ops[i]["dur"]
        end[i] = est[i] + ops[i]["dur"] + ops[i]["lat"]
        for u in users[i]:
            left[u] -= 1
            early[u] = max(early[u], end[i] + WAKE + dict(ops[u]["after"]).get(i, 0))
            if left[u] == 0:
                ready.append(u)

    count, known, clock, token = {}, {q: {} for q in Q}, {}, {}
    for _, _, i in order:
        o, q = ops[i], ops[i]["q"]
        if o["kind"] == "land":
            token[i] = (o["sem"], o["n"])
            clock[token[i]] = {o["sem"]: o["n"]}
            total[o["sem"]] = o["n"]
            continue
        toks = {}
        for d in o["deps"]:
            if d in token:
                toks[token[d][0]] = max(toks.get(token[d][0], 0), token[d][1])
        todo = [t for t in toks.items() if known[q].get(t[0], 0) < t[1]]
        for t in sorted(t for t in todo if not any(u != t and clock[u].get(t[0], 0) >= t[1] for u in todo)):
            Q[q].wait_ge(T.sem[t[0]], t[1])
            for a, b in clock[t].items():
                known[q][a] = max(known[q].get(a, 0), b)
        ins = o["fn"]()
        if o["kind"] == "send":
            continue
        s = o["sem"] or SEM[q]
        count[s] = total[s] = count.get(s, 0) + o["n"]
        ins.then_inc(T.sem[s], o["n"])
        token[i] = (s, count[s])
        clock[token[i]] = dict(known[q])
        clock[token[i]][s] = count[s]
    for s in sorted(total):
        g.wait_ge(T.sem[s], total[s])
